import numpy as np
import ml_dtypes


def mxq(x, axis, fmt="e4m3"):
    dtype, down = {"e4m3": (ml_dtypes.float8_e4m3fn, 7), "e5m2": (ml_dtypes.float8_e5m2, 14)}[fmt]
    v = np.moveaxis(np.asarray(x, np.float32).astype(ml_dtypes.bfloat16).astype(np.float64), axis, -1)
    blocks = v.reshape(v.shape[:-1] + (-1, 32))
    amax = np.abs(blocks).max(-1, keepdims=True)
    byte = np.maximum(np.where(amax > 0, np.frexp(amax)[1] - 1 + 127, 0) - down, 1)
    scale = np.exp2(byte - 127.0)
    codes = (blocks / scale).astype(np.float32).astype(dtype).astype(np.float64)
    return np.moveaxis((codes * scale).reshape(v.shape), -1, axis)


WIDE = False


def mx_kscale(k):
    if not WIDE:
        return np.ones(k)
    levels = np.array([10, -10, 5, -5, 0])
    if k % 512:
        return np.exp2(np.random.permutation(np.resize(levels, k // 32))).repeat(32)
    a = np.empty((k // 512, 16))
    for p in range(k // 512):
        a[p, :8] = np.random.permutation(np.resize(levels, 8))
        for g in range(8):
            far = levels[np.abs(levels - a[p, g]) >= 10]
            a[p, g + 8] = far[np.random.randint(len(far))]
    return np.exp2(a.ravel()).repeat(32)


def f64(x):
    return np.asarray(x).astype(np.float64)


def striped(idx):
    return np.tile(idx.reshape(-1, 16).T, (8, 1)).astype(np.uint16)


def unstriped(offs):
    return offs[:16].T.reshape(-1).astype(np.int64)


E2M1 = np.array([0.0, 0.5, 1.0, 1.5, 2.0, 3.0, 4.0, 6.0, -0.0, -0.5, -1.0, -1.5, -2.0, -3.0, -4.0, -6.0])


def pack_weight(w, fmt):
    k, n = w.shape
    w = f64(np.asarray(w, np.float32).astype(ml_dtypes.bfloat16)).reshape(k // 32, 32, n)
    amax = np.abs(w).max(1)
    if fmt == "e4m3":
        byte = np.frexp(amax)[1] - 1 + 127 - 7
    else:
        mant, ex = np.frexp(amax / 6.0)
        byte = np.where(mant > 0.5, ex, ex - 1) + 127
    byte = np.clip(np.where(amax > 0, byte, 1), 1, 254)
    scaled = (w * np.exp2(127.0 - byte)[:, None, :]).reshape(k, n).astype(np.float32)
    by_word = np.ascontiguousarray(scaled.reshape(k // 512, 128, 4, n).transpose(0, 1, 3, 2))
    if fmt == "e4m3":
        words = by_word.astype(ml_dtypes.float8_e4m3fn).view(np.uint8)
    else:
        c = by_word.astype(ml_dtypes.float4_e2m1fn).view(np.uint8) & 0xF
        words = (c[..., 0::2] | (c[..., 1::2] << 4)).reshape(k // 512, 128, 2 * n)
    return np.ascontiguousarray(words), np.ascontiguousarray(byte.astype(np.uint8).reshape(k // 512, 16, n))


def unpack_weight(words, scales, fmt):
    g, _, n = scales.shape
    words = np.ascontiguousarray(words).reshape(g, 128, n, -1)
    if fmt == "e4m3":
        vals = words.view(ml_dtypes.float8_e4m3fn).astype(np.float64)
    else:
        nib = np.empty((g, 128, n, 4), np.uint8)
        nib[..., 0::2] = words & 0xF
        nib[..., 1::2] = words >> 4
        vals = E2M1[nib]
    vals = vals * np.repeat(np.exp2(scales.astype(np.float64) - 127.0), 8, axis=1)[..., None]
    return vals.transpose(0, 1, 3, 2).reshape(g * 512, n)


K, T, E, C, N = 2560, 384, 12, 128, 256
TOP = 4
K8 = 1024


def by_expert(wq, xq):
    return np.concatenate([wq[e].T @ xq[:, e * C:(e + 1) * C] for e in range(E)], axis=1)


def setup_inputs():
    n = np.random.standard_normal
    s = mx_kscale(K)[:, None]
    deal = np.repeat(np.arange(E), C).reshape(TOP, T)[:, np.random.permutation(T)]
    deal = np.take_along_axis(deal, np.argsort(np.random.rand(TOP, T), axis=0), axis=0)
    for _ in range(8):
        s_, t_ = np.random.permutation(T).reshape(2, -1); r = np.random.randint(TOP, size=T // 2); x, y = deal[r, s_].copy(), deal[r, t_].copy()
        ok = ~((deal[:, s_] == y).any(0) | (deal[:, t_] == x).any(0)); deal[r[ok], s_[ok]] = y[ok]; deal[r[ok], t_[ok]] = x[ok]
    order = np.lexsort((np.random.rand(TOP * T), deal.reshape(-1)))
    slot_token = order % T; pos = np.empty(TOP * T, np.int64); pos[order] = np.arange(TOP * T); pos = pos.reshape(TOP, T)
    g = np.random.uniform(0.5, 1.5, (TOP, T)); g = g / g.sum(0)
    w = n((E, K, N)) / np.sqrt(K) / s[None]
    w8 = [pack_weight(m[:K8], "e4m3") for m in w]
    w4 = [pack_weight(m[K8:], "e2m1") for m in w]
    return {
        "xT": (n((K, T)) * s).astype(np.float32),
        "w8_words": np.stack([m[0] for m in w8]),
        "w8_scales": np.stack([m[1] for m in w8]),
        "w4_words": np.stack([m[0] for m in w4]),
        "w4_scales": np.stack([m[1] for m in w4]),
        "gate": np.stack([np.tile(r, (N, 1)) for r in g]).astype(np.float32),
        "offs": striped(slot_token),
        "pos1": striped(pos[0]),
        "pos2": striped(pos[1]),
        "pos3": striped(pos[2]),
        "pos4": striped(pos[3]),
    }


def reference(xT, w8_words, w8_scales, w4_words, w4_scales, gate, offs, pos1, pos2, pos3, pos4):
    idx = unstriped(offs)
    w = np.stack([np.concatenate([unpack_weight(w8_words[e], w8_scales[e], "e4m3"), unpack_weight(w4_words[e], w4_scales[e], "e2m1")]) for e in range(E)])
    xq = mxq(f64(xT)[:, idx], 0, "e4m3")
    y = by_expert(w, xq)
    return sum(f64(gate[r]) * y[:, unstriped(p)] for r, p in enumerate((pos1, pos2, pos3, pos4)))

@@ -1,0 +1,203 @@
+from contextlib import ExitStack
+
+import concourse.mybir as mybir
+
+F32 = mybir.dt.float32
+BF16 = mybir.dt.bfloat16
+I32 = mybir.dt.int32
+U32 = mybir.dt.uint32
+U16 = mybir.dt.uint16
+U8 = mybir.dt.uint8
+FP8X4 = mybir.dt.float8_e4m3fn_x4
+FP4X4 = mybir.dt.float4_e2m1fn_x4
+COPY = mybir.ActivationFunctionType.Copy
+MULT = mybir.AluOpType.mult
+ADD = mybir.AluOpType.add
+
+P = 128
+K, T, E, C, N = 2560, 384, 12, 128, 256
+TOP = 4
+SLOTS = E * C
+PASSES = 5
+PASSES8 = 2
+PASSES4 = 3
+HALVES = N // P
+GROUP = 384
+GROUPS = SLOTS // GROUP
+W_EXPERTS = E // GROUPS
+WINDOW = 512
+FLOPS = 2 * SLOTS * K * N
+
+PLANES = 3
+PLACE = {2: (0, 0), 0: (0, 4), 1: (0, 8), 3: (1, 0), 4: (2, 0)}
+CUTS = (0, 256, 512, 896, 1280, 1408, 1536)
+
+
+def tile_moe_tk_lin_none_kernel(
+    tc, xT, w8_words, w8_scales, w4_words, w4_scales, gate, offs, pos1, pos2, pos3, pos4, out
+):
+    nc = tc.nc
+    with ExitStack() as ctx:
+        keep = ctx.enter_context(tc.tile_pool(name="keep", bufs=1))
+        psum = ctx.enter_context(tc.psum_pool(name="psum", bufs=8))
+
+        def tile(shape, dtype, name, tag=""):
+            return keep.tile(shape, dtype, name=name, tag=tag or name, align_bytes=64)
+
+        offs_list = keep.tile([P, SLOTS // 16], U16, name="offs_list")
+        pos_lists = [keep.tile([P, T // 16], U16, name="pos%d_list" % r) for r in range(TOP)]
+
+        raw = [tile([P, 4, T], F32, "raw%d" % a) for a in range(PASSES)]
+        big = [tile([P, 256, 4], BF16, "big%d" % a) for a in range(PASSES)]
+        small = [tile([P, 128, 4], BF16, "small%d" % a) for a in range(PASSES)]
+        codes = [tile([P, WINDOW], U32, "codes%d" % a) for a in range(PASSES)]
+        words = [tile([P, SLOTS], U32, "words%d" % a) for a in range(PASSES)]
+        planes = [tile([P, WINDOW], U8, "planes%d" % i) for i in range(PLANES)]
+        bytes_g = [tile([P, SLOTS], U8, "bytes%d" % i) for i in range(PLANES)]
+        stage = tile([16, E * PASSES, N], U8, "stage")
+        scales = tile([P, E * PASSES, N], U8, "scales")
+        w8 = [tile([P, W_EXPERTS * PASSES8, 4 * N], U8, "w8_%d" % g) for g in range(GROUPS)]
+        w4 = [tile([P, W_EXPERTS * PASSES4, 2 * N], U8, "w4_%d" % g) for g in range(GROUPS)]
+        gates = [tile([P, TOP, T], F32, "gates%d" % h) for h in range(HALVES)]
+        y = [tile([P, SLOTS], F32, "y%d" % h) for h in range(HALVES)]
+        prod = [tile([P, TOP, T], F32, "prod%d" % h) for h in range(HALVES)]
+        part = [tile([P, 2, T], F32, "part%d" % h) for h in range(HALVES)]
+        res = [tile([P, T], F32, "res%d" % h) for h in range(HALVES)]
+
+        def load_x(a, lo, hi):
+            rows = xT[512 * a : 512 * (a + 1), :].rearrange("(p j) w -> p j w", j=4)
+            nc.sync.dma_start(raw[a][:, :, lo:hi], rows[:, :, lo:hi])
+
+        def turn(dst, a, lo, hi, on_vector=False):
+            src = raw[a][:, :, lo:hi].rearrange("p j w -> p w j")
+            if on_vector:
+                nc.vector.tensor_copy(out=dst[:], in_=src)
+            else:
+                nc.scalar.activation(dst[:], src, COPY)
+
+        def quantise(a):
+            i, row = PLACE[a]
+            for src, lo, hi in ((big[a], 0, 256), (small[a], 256, T)):
+                nc.vector.quantize_mx(
+                    out=codes[a][:, lo:hi].bitcast(FP8X4),
+                    scales=planes[i][row:P, lo:hi],
+                    in_=src[:].rearrange("p w j -> p (w j)"),
+                )
+
+        def gather_words(a, lo, hi):
+            nc.vector.tensor_copy(
+                out=words[a][:, lo:hi], in_=codes[a][:].indirect(offs_list[:, lo // 16 : hi // 16])
+            )
+
+        def gather_bytes(i, lo, hi):
+            nc.vector.tensor_copy(
+                out=bytes_g[i][:, lo:hi], in_=planes[i][:].indirect(offs_list[:, lo // 16 : hi // 16])
+            )
+
+        nc.sync.dma_start(offs_list[:], offs)
+        load_x(4, 0, 256)
+        load_x(4, 256, T)
+        load_x(3, 0, T)
+        n8 = E * PASSES8
+        nc.sync.dma_start(stage[:, 0:n8, :].bitcast(I32), w8_scales.rearrange("e a q n -> q (e a) n").bitcast(I32))
+        nc.sync.dma_start(stage[:, n8:, :].bitcast(I32), w4_scales.rearrange("e a q n -> q (e a) n").bitcast(I32))
+        for a in (2, 0, 1):
+            load_x(a, 0, T)
+        for q in range(4):
+            nc.sync.dma_start(
+                scales[32 * q : 32 * q + 4, :, :].bitcast(I32), stage[4 * q : 4 * q + 4, :, :].bitcast(I32)
+            )
+        for g in range(GROUPS):
+            ee = slice(W_EXPERTS * g, W_EXPERTS * (g + 1))
+            nc.sync.dma_start(
+                w8[g][:].bitcast(I32), w8_words[ee].rearrange("e a p n r -> p (e a) (n r)").bitcast(I32)
+            )
+            nc.sync.dma_start(w4[g][:].bitcast(I32), w4_words[ee].rearrange("e a p b -> p (e a) b").bitcast(I32))
+        for r, pos in enumerate((pos1, pos2, pos3, pos4)):
+            nc.sync.dma_start(pos_lists[r][:], pos)
+        for h in range(HALVES):
+            nc.sync.dma_start(gates[h][:], gate[:, P * h : P * (h + 1), :].rearrange("r p t -> p r t"))
+
+        for t in planes:
+            nc.vector.memset(t[:].bitcast(I32), 0)
+        for a in (4, 3, 2, 0, 1):
+            nc.vector.memset(codes[a][:, T:WINDOW].bitcast(I32), 0)
+
+        turn(big[4], 4, 0, 256, on_vector=True)
+        turn(small[4], 4, 256, T)
+        for a in (3, 2, 0, 1):
+            turn(big[a], a, 0, 256)
+            turn(small[a], a, 256, T)
+        for a in (4, 3, 2):
+            quantise(a)
+            for lo in range(0, SLOTS, GROUP):
+                gather_words(a, lo, lo + GROUP)
+            if a != 2:
+                for lo in range(0, SLOTS, GROUP):
+                    gather_bytes(PLACE[a][0], lo, lo + GROUP)
+        quantise(0)
+        quantise(1)
+        for lo, hi in zip(CUTS, CUTS[1:]):
+            gather_bytes(0, lo, hi)
+            gather_words(0, lo, hi)
+            gather_words(1, lo, hi)
+
+        def step(acc, e, h, a, col, first, last):
+            g, ee = divmod(e, W_EXPERTS)
+            ch = slice(P * h, P * (h + 1))
+            s = slice(C * e, C * (e + 1))
+            if a < PASSES8:
+                lhsT = w8[g][:, PASSES8 * ee + a, 4 * P * h : 4 * P * (h + 1)].bitcast(FP8X4)
+                lhsT_scale = scales[:, PASSES8 * e + a, ch]
+            else:
+                lhsT = w4[g][:, PASSES4 * ee + a - PASSES8, 2 * P * h : 2 * P * (h + 1)].bitcast(FP4X4)
+                lhsT_scale = scales[:, n8 + PASSES4 * e + a - PASSES8, ch]
+            i, row = PLACE[a]
+            nc.tensor.matmul_mx(
+                out=acc[:, C * col : C * (col + 1)],
+                lhsT=lhsT,
+                lhsT_scale=lhsT_scale,
+                rhs=words[a][:, s].bitcast(FP8X4),
+                rhs_scale=bytes_g[i][row:P, s],
+                start=first,
+                stop=last,
+            )
+
+        def bank():
+            return psum.tile([P, WINDOW], F32, name="bank")
+
+        def empty(acc, h, experts):
+            nc.scalar.activation(
+                y[h][:, C * experts[0] : C * (experts[-1] + 1)], acc[:, 0 : C * len(experts)], COPY
+            )
+
+        first_wave = [(e, h, bank()) for e in range(4) for h in range(HALVES)]
+        for e, h, acc in first_wave:
+            for a in (4, 3):
+                step(acc, e, h, a, 0, a == 4, False)
+        for e, h, acc in first_wave:
+            for a in (2, 0, 1):
+                step(acc, e, h, a, 0, False, a == 1)
+            empty(acc, h, (e,))
+        for h in range(HALVES):
+            for experts in ((4, 5, 6), (7, 8, 9), (10,), (11,)):
+                acc = bank()
+                for col, e in enumerate(experts):
+                    for a in (4, 3, 2, 0, 1):
+                        step(acc, e, h, a, col, a == 4, a == 1)
+                empty(acc, h, experts)
+
+        def fetch(h, r):
+            nc.vector.tensor_tensor(
+                prod[h][:, r, :], y[h][:].indirect(pos_lists[r][:]), gates[h][:, r, :], MULT
+            )
+
+        for h in range(HALVES):
+            fetch(h, 0)
+            fetch(h, 1)
+            fetch(h, 2)
+            nc.vector.tensor_tensor(part[h][:, 0, :], prod[h][:, 0, :], prod[h][:, 1, :], ADD)
+            fetch(h, 3)
+            nc.vector.tensor_tensor(part[h][:, 1, :], part[h][:, 0, :], prod[h][:, 2, :], ADD)
+            nc.vector.tensor_tensor(res[h][:], part[h][:, 1, :], prod[h][:, 3, :], ADD)
+            nc.sync.dma_start(out[P * h : P * (h + 1), :], res[h][:])

@@ -22,15 +22,15 @@ PASSES = 5
 PASSES8 = 2
 PASSES4 = 3
 HALVES = N // P
-GROUP = 384
-GROUPS = SLOTS // GROUP
-W_EXPERTS = E // GROUPS
-WINDOW = 512
 FLOPS = 2 * SLOTS * K * N
 
-PLANES = 3
-PLACE = {2: (0, 0), 0: (0, 4), 1: (0, 8), 3: (1, 0), 4: (2, 0)}
-CUTS = (0, 256, 512, 896, 1280, 1408, 1536)
+ORDER = (2, 0, 1, 4, 3)
+SUM_ORDER = (2, 0, 1, 3, 4)
+WIDE = 2048
+PLACE = {2: (1, 0), 0: (1, 4), 1: (1, 8), 4: (1, 12), 3: (0, 0)}
+PLANES = 2
+MOVED = 4
+BANKS = ((0, 1, 2, 3), (4, 5, 6, 7), (8, 9, 10), (11,))
 
 
 def tile_moe_tk_lin_none_kernel(
@@ -50,23 +50,32 @@ def tile_moe_tk_lin_none_kernel(
         raw = [tile([P, 4, T], F32, "raw%d" % a) for a in range(PASSES)]
         big = [tile([P, 256, 4], BF16, "big%d" % a) for a in range(PASSES)]
         small = [tile([P, 128, 4], BF16, "small%d" % a) for a in range(PASSES)]
-        codes = [tile([P, WINDOW], U32, "codes%d" % a) for a in range(PASSES)]
-        words = [tile([P, SLOTS], U32, "words%d" % a) for a in range(PASSES)]
-        planes = [tile([P, WINDOW], U8, "planes%d" % i) for i in range(PLANES)]
+        codes = tile([P, (PASSES - 1) * T + WIDE], U32, "codes")
+        planes = tile([P, (PLANES - 1) * T + WIDE], U8, "planes")
+        words = [tile([P, SLOTS], U32, "words%d" % a) for a in range(PASSES - 1)]
         bytes_g = [tile([P, SLOTS], U8, "bytes%d" % i) for i in range(PLANES)]
-        stage = tile([16, E * PASSES, N], U8, "stage")
-        scales = tile([P, E * PASSES, N], U8, "scales")
-        w8 = [tile([P, W_EXPERTS * PASSES8, 4 * N], U8, "w8_%d" % g) for g in range(GROUPS)]
-        w4 = [tile([P, W_EXPERTS * PASSES4, 2 * N], U8, "w4_%d" % g) for g in range(GROUPS)]
-        gates = [tile([P, TOP, T], F32, "gates%d" % h) for h in range(HALVES)]
+        moved = tile([P, SLOTS], U8, "moved")
+        s4 = tile([P, E * PASSES4, N], U8, "s4")
+        s8 = tile([P, E, N], U8, "s8")
+        w = [tile([P, E, (4 if a < PASSES8 else 2) * N], U8, "w%d" % a) for a in range(PASSES)]
         y = [tile([P, SLOTS], F32, "y%d" % h) for h in range(HALVES)]
         prod = [tile([P, TOP, T], F32, "prod%d" % h) for h in range(HALVES)]
         part = [tile([P, 2, T], F32, "part%d" % h) for h in range(HALVES)]
         res = [tile([P, T], F32, "res%d" % h) for h in range(HALVES)]
 
+        def home(a):
+            return T * (PASSES - 1 - ORDER.index(a))
+
         def load_x(a, lo, hi):
             rows = xT[512 * a : 512 * (a + 1), :].rearrange("(p j) w -> p j w", j=4)
             nc.sync.dma_start(raw[a][:, :, lo:hi], rows[:, :, lo:hi])
+
+        def load_w(a, lo, hi):
+            if a < PASSES8:
+                src = w8_words[lo:hi, a].rearrange("e p n r -> p e (n r)")
+            else:
+                src = w4_words[lo:hi, a - PASSES8].rearrange("e p b -> p e b")
+            nc.sync.dma_start(w[a][:, lo:hi, :].bitcast(I32), src.bitcast(I32))
 
         def turn(dst, a, lo, hi, on_vector=False):
             src = raw[a][:, :, lo:hi].rearrange("p j w -> p w j")
@@ -79,118 +88,126 @@ def tile_moe_tk_lin_none_kernel(
             i, row = PLACE[a]
             for src, lo, hi in ((big[a], 0, 256), (small[a], 256, T)):
                 nc.vector.quantize_mx(
-                    out=codes[a][:, lo:hi].bitcast(FP8X4),
-                    scales=planes[i][row:P, lo:hi],
+                    out=codes[:, home(a) + lo : home(a) + hi].bitcast(FP8X4),
+                    scales=planes[row:P, T * i + lo : T * i + hi],
                     in_=src[:].rearrange("p w j -> p (w j)"),
                 )
 
+        def width(count):
+            return 512 if count <= 384 else 1024 if count <= 768 else WIDE
+
         def gather_words(a, lo, hi):
-            nc.vector.tensor_copy(
-                out=words[a][:, lo:hi], in_=codes[a][:].indirect(offs_list[:, lo // 16 : hi // 16])
-            )
+            window = codes[:, home(a) : home(a) + width(hi - lo)]
+            nc.vector.tensor_copy(out=words[a][:, lo:hi], in_=window.indirect(offs_list[:, lo // 16 : hi // 16]))
 
         def gather_bytes(i, lo, hi):
-            nc.vector.tensor_copy(
-                out=bytes_g[i][:, lo:hi], in_=planes[i][:].indirect(offs_list[:, lo // 16 : hi // 16])
-            )
+            window = planes[:, T * i : T * i + width(hi - lo)]
+            nc.vector.tensor_copy(out=bytes_g[i][:, lo:hi], in_=window.indirect(offs_list[:, lo // 16 : hi // 16]))
 
+        load_x(2, 0, 256)
+        load_x(2, 256, T)
         nc.sync.dma_start(offs_list[:], offs)
-        load_x(4, 0, 256)
-        load_x(4, 256, T)
-        load_x(3, 0, T)
-        n8 = E * PASSES8
-        nc.sync.dma_start(stage[:, 0:n8, :].bitcast(I32), w8_scales.rearrange("e a q n -> q (e a) n").bitcast(I32))
-        nc.sync.dma_start(stage[:, n8:, :].bitcast(I32), w4_scales.rearrange("e a q n -> q (e a) n").bitcast(I32))
-        for a in (2, 0, 1):
-            load_x(a, 0, T)
-        for q in range(4):
-            nc.sync.dma_start(
-                scales[32 * q : 32 * q + 4, :, :].bitcast(I32), stage[4 * q : 4 * q + 4, :, :].bitcast(I32)
-            )
-        for g in range(GROUPS):
-            ee = slice(W_EXPERTS * g, W_EXPERTS * (g + 1))
-            nc.sync.dma_start(
-                w8[g][:].bitcast(I32), w8_words[ee].rearrange("e a p n r -> p (e a) (n r)").bitcast(I32)
-            )
-            nc.sync.dma_start(w4[g][:].bitcast(I32), w4_words[ee].rearrange("e a p b -> p (e a) b").bitcast(I32))
+        load_x(0, 0, T)
+        load_x(1, 0, T)
+        load_x(4, 0, T)
         for r, pos in enumerate((pos1, pos2, pos3, pos4)):
             nc.sync.dma_start(pos_lists[r][:], pos)
-        for h in range(HALVES):
-            nc.sync.dma_start(gates[h][:], gate[:, P * h : P * (h + 1), :].rearrange("r p t -> p r t"))
+        for r in range(4):
+            nc.sync.dma_start(
+                s4[r:P:32, :, :].bitcast(I32),
+                w4_scales.rearrange("e a (q r) n -> r q (e a) n", r=4)[r].bitcast(I32),
+            )
+        for a in range(PASSES8):
+            for r in range(4):
+                nc.sync.dma_start(
+                    s8[PLACE[a][1] + r : P : 32, :, :].bitcast(I32),
+                    w8_scales[:, a].rearrange("e (q r) n -> r q e n", r=4)[r].bitcast(I32),
+                )
+        load_x(3, 0, T)
+        for a in SUM_ORDER:
+            load_w(a, 0, E)
 
-        for t in planes:
-            nc.vector.memset(t[:].bitcast(I32), 0)
-        for a in (4, 3, 2, 0, 1):
-            nc.vector.memset(codes[a][:, T:WINDOW].bitcast(I32), 0)
+        nc.vector.memset(planes[:].bitcast(I32), 0)
+        nc.vector.memset(codes[:, PASSES * T :].bitcast(I32), 0)
 
-        turn(big[4], 4, 0, 256, on_vector=True)
-        turn(small[4], 4, 256, T)
-        for a in (3, 2, 0, 1):
+        banks = {}
+        for b in range(len(BANKS)):
+            for h in range(HALVES):
+                banks[b, h] = psum.tile([P, 512], F32, name="bank")
+
+        def step(b, h, a):
+            ch = slice(P * h, P * (h + 1))
+            i, row = PLACE[a]
+            for col, e in enumerate(BANKS[b]):
+                s = slice(C * e, C * (e + 1))
+                if a < PASSES8:
+                    lhsT = w[a][:, e, 4 * P * h : 4 * P * (h + 1)].bitcast(FP8X4)
+                    lhsT_scale = s8[row:P, e, ch]
+                else:
+                    lhsT = w[a][:, e, 2 * P * h : 2 * P * (h + 1)].bitcast(FP4X4)
+                    lhsT_scale = s4[:, PASSES4 * e + a - PASSES8, ch]
+                nc.tensor.matmul_mx(
+                    out=banks[b, h][:, C * col : C * (col + 1)],
+                    lhsT=lhsT,
+                    lhsT_scale=lhsT_scale,
+                    rhs=words[a][:, s].bitcast(FP8X4),
+                    rhs_scale=moved[:, s] if a == MOVED else bytes_g[i][row:P, s],
+                    start=(a == SUM_ORDER[0] and col == 0),
+                    stop=(a == SUM_ORDER[-1] and e == BANKS[b][-1]),
+                )
+
+        def products(a):
+            for b in range(len(BANKS)):
+                for h in range(HALVES):
+                    step(b, h, a)
+
+        def empty(b, h, on_vector=False):
+            dst = y[h][:, C * BANKS[b][0] : C * (BANKS[b][-1] + 1)]
+            src = banks[b, h][:, 0 : C * len(BANKS[b])]
+            if on_vector:
+                nc.vector.tensor_copy(out=dst, in_=src)
+            else:
+                nc.scalar.activation(dst, src, COPY)
+
+        turn(big[2], 2, 0, 256, on_vector=True)
+        turn(small[2], 2, 256, T)
+        for a in ORDER[1:]:
             turn(big[a], a, 0, 256)
             turn(small[a], a, 256, T)
-        for a in (4, 3, 2):
+        for a in (2, 0):
             quantise(a)
-            for lo in range(0, SLOTS, GROUP):
-                gather_words(a, lo, lo + GROUP)
-            if a != 2:
-                for lo in range(0, SLOTS, GROUP):
-                    gather_bytes(PLACE[a][0], lo, lo + GROUP)
-        quantise(0)
+            gather_words(a, 0, SLOTS)
         quantise(1)
-        for lo, hi in zip(CUTS, CUTS[1:]):
-            gather_bytes(0, lo, hi)
-            gather_words(0, lo, hi)
-            gather_words(1, lo, hi)
-
-        def step(acc, e, h, a, col, first, last):
-            g, ee = divmod(e, W_EXPERTS)
-            ch = slice(P * h, P * (h + 1))
-            s = slice(C * e, C * (e + 1))
-            if a < PASSES8:
-                lhsT = w8[g][:, PASSES8 * ee + a, 4 * P * h : 4 * P * (h + 1)].bitcast(FP8X4)
-                lhsT_scale = scales[:, PASSES8 * e + a, ch]
-            else:
-                lhsT = w4[g][:, PASSES4 * ee + a - PASSES8, 2 * P * h : 2 * P * (h + 1)].bitcast(FP4X4)
-                lhsT_scale = scales[:, n8 + PASSES4 * e + a - PASSES8, ch]
-            i, row = PLACE[a]
-            nc.tensor.matmul_mx(
-                out=acc[:, C * col : C * (col + 1)],
-                lhsT=lhsT,
-                lhsT_scale=lhsT_scale,
-                rhs=words[a][:, s].bitcast(FP8X4),
-                rhs_scale=bytes_g[i][row:P, s],
-                start=first,
-                stop=last,
+        quantise(4)
+        gather_bytes(1, 0, SLOTS)
+        for r in range(4):
+            nc.sync.dma_start(
+                moved[r:P:32, :].bitcast(I32), bytes_g[1][PLACE[MOVED][1] + r : P : 32, :].bitcast(I32)
             )
-
-        def bank():
-            return psum.tile([P, WINDOW], F32, name="bank")
-
-        def empty(acc, h, experts):
-            nc.scalar.activation(
-                y[h][:, C * experts[0] : C * (experts[-1] + 1)], acc[:, 0 : C * len(experts)], COPY
-            )
-
-        first_wave = [(e, h, bank()) for e in range(4) for h in range(HALVES)]
-        for e, h, acc in first_wave:
-            for a in (4, 3):
-                step(acc, e, h, a, 0, a == 4, False)
-        for e, h, acc in first_wave:
-            for a in (2, 0, 1):
-                step(acc, e, h, a, 0, False, a == 1)
-            empty(acc, h, (e,))
-        for h in range(HALVES):
-            for experts in ((4, 5, 6), (7, 8, 9), (10,), (11,)):
-                acc = bank()
-                for col, e in enumerate(experts):
-                    for a in (4, 3, 2, 0, 1):
-                        step(acc, e, h, a, col, a == 4, a == 1)
-                empty(acc, h, experts)
+        products(2)
+        products(0)
+        gather_words(1, 0, SLOTS)
+        products(1)
+        quantise(3)
+        gates = tile([P, TOP, T], F32, "gates", tag="big3")
+        nc.sync.dma_start(gates[:], gate[:, 0:P, :].rearrange("r p t -> p r t"))
+        gather_bytes(0, 0, SLOTS)
+        gather_words(3, 0, SLOTS)
+        products(3)
+        words.append(tile([P, SLOTS], U32, "words4", tag="planes"))
+        for b, experts in enumerate(BANKS):
+            gather_words(4, C * experts[0], C * (experts[-1] + 1))
+            for h in range(HALVES):
+                step(b, h, 4)
+        last = len(BANKS) - 1
+        for b in range(last):
+            empty(b, 0)
+        empty(last, 0, on_vector=True)
+        for b in range(len(BANKS)):
+            empty(b, 1)
 
         def fetch(h, r):
-            nc.vector.tensor_tensor(
-                prod[h][:, r, :], y[h][:].indirect(pos_lists[r][:]), gates[h][:, r, :], MULT
-            )
+            nc.vector.tensor_tensor(prod[h][:, r, :], y[h][:].indirect(pos_lists[r][:]), gates[:, r, :], MULT)
 
         for h in range(HALVES):
             fetch(h, 0)

@@ -1,6 +1,7 @@
 from contextlib import ExitStack
 
 import concourse.mybir as mybir
+from concourse.masks import make_identity
 
 F32 = mybir.dt.float32
 BF16 = mybir.dt.bfloat16
@@ -60,7 +61,8 @@ def tile_moe_tk_lin_none_kernel(
         w = [tile([P, E, (4 if a < PASSES8 else 2) * N], U8, "w%d" % a) for a in range(PASSES)]
         y = [tile([P, SLOTS], F32, "y%d" % h) for h in range(HALVES)]
         prod = [tile([P, TOP, T], F32, "prod%d" % h) for h in range(HALVES)]
-        part = [tile([P, 2, T], F32, "part%d" % h) for h in range(HALVES)]
+        turned = [tile([P, T], F32, "turned%d" % h) for h in range(HALVES)]
+        ident = tile([P, P], F32, "ident")
         res = [tile([P, T], F32, "res%d" % h) for h in range(HALVES)]
 
         def home(a):
@@ -127,6 +129,7 @@ def tile_moe_tk_lin_none_kernel(
         for a in SUM_ORDER:
             load_w(a, 0, E)
 
+        make_identity(nc, ident[:])
         nc.vector.memset(planes[:].bitcast(I32), 0)
         nc.vector.memset(codes[:, PASSES * T :].bitcast(I32), 0)
 
@@ -209,12 +212,26 @@ def tile_moe_tk_lin_none_kernel(
         def fetch(h, r):
             nc.vector.tensor_tensor(prod[h][:, r, :], y[h][:].indirect(pos_lists[r][:]), gates[:, r, :], MULT)
 
+        blocks = T // P
+        back = []
         for h in range(HALVES):
-            fetch(h, 0)
-            fetch(h, 1)
-            fetch(h, 2)
-            nc.vector.tensor_tensor(part[h][:, 0, :], prod[h][:, 0, :], prod[h][:, 1, :], ADD)
-            fetch(h, 3)
-            nc.vector.tensor_tensor(part[h][:, 1, :], part[h][:, 0, :], prod[h][:, 2, :], ADD)
-            nc.vector.tensor_tensor(res[h][:], part[h][:, 1, :], prod[h][:, 3, :], ADD)
+            there = psum.tile([P, 512], F32, name="bank")
+            for r in range(TOP - 1):
+                fetch(h, r)
+                for b in range(blocks):
+                    nc.tensor.matmul(
+                        there[:, P * b : P * (b + 1)],
+                        prod[h][:, r, P * b : P * (b + 1)],
+                        ident[:],
+                        start=(r == 0 and b == 0),
+                        stop=(r == TOP - 2 and b == blocks - 1),
+                        is_transpose=True,
+                    )
+            nc.scalar.activation(turned[h][:], there[:, 0:T], COPY)
+            back.append(psum.tile([P, 512], F32, name="bank"))
+            for b in range(blocks):
+                nc.tensor.transpose(back[h][:, P * b : P * (b + 1)], turned[h][:, P * b : P * (b + 1)], ident[:])
+        for h in range(HALVES):
+            fetch(h, TOP - 1)
+            nc.vector.tensor_tensor(res[h][:], back[h][:, 0:T], prod[h][:, TOP - 1, :], ADD)
             nc.sync.dma_start(out[P * h : P * (h + 1), :], res[h][:])

@@ -31,6 +31,7 @@ WIDE = 2048
 PLACE = {2: (1, 0), 0: (1, 4), 1: (1, 8), 4: (1, 12), 3: (0, 0)}
 PLANES = 2
 MOVED = 4
+S8_ROW = 8
 BANKS = ((0, 1, 2, 3), (4, 5, 6, 7), (8, 9, 10), (11,))
 
 
@@ -53,14 +54,14 @@ def tile_moe_tk_lin_none_kernel(
         small = [tile([P, 128, 4], BF16, "small%d" % a) for a in range(PASSES)]
         codes = tile([P, (PASSES - 1) * T + WIDE], U32, "codes")
         planes = tile([P, (PLANES - 1) * T + WIDE], U8, "planes")
-        words = [tile([P, SLOTS], U32, "words%d" % a) for a in range(PASSES - 1)]
-        bytes_g = [tile([P, SLOTS], U8, "bytes%d" % i) for i in range(PLANES)]
+        words = {a: tile([P, SLOTS], U32, "words%d" % a) for a in (2, 3)}
+        bytes_g = {0: tile([P, SLOTS], U8, "bytes0")}
         moved = tile([P, SLOTS], U8, "moved")
         s4 = tile([P, E * PASSES4, N], U8, "s4")
-        s8 = tile([P, E, N], U8, "s8")
+        s8 = tile([P, E * PASSES8, N], U8, "s8")
         w = [tile([P, E, (4 if a < PASSES8 else 2) * N], U8, "w%d" % a) for a in range(PASSES)]
         y = [tile([P, SLOTS], F32, "y%d" % h) for h in range(HALVES)]
-        prod = [tile([P, TOP, T], F32, "prod%d" % h) for h in range(HALVES)]
+        prod = [tile([P, TOP - 1, T], F32, "prod%d" % h) for h in range(HALVES)]
         turned = [tile([P, T], F32, "turned%d" % h) for h in range(HALVES)]
         ident = tile([P, P], F32, "ident")
         res = [tile([P, T], F32, "res%d" % h) for h in range(HALVES)]
@@ -71,6 +72,14 @@ def tile_moe_tk_lin_none_kernel(
         def load_x(a, lo, hi):
             rows = xT[512 * a : 512 * (a + 1), :].rearrange("(p j) w -> p j w", j=4)
             nc.sync.dma_start(raw[a][:, :, lo:hi], rows[:, :, lo:hi])
+
+        def load_s4(r):
+            src = w4_scales.rearrange("e a (q r) n -> r q (e a) n", r=4)[r]
+            nc.sync.dma_start(s4[r:P:32, :, :].bitcast(I32), src.bitcast(I32))
+
+        def load_s8(r):
+            src = w8_scales.rearrange("e a (q r) n -> r q (e a) n", r=4)[r]
+            nc.sync.dma_start(s8[S8_ROW + r : P : 32, :, :].bitcast(I32), src.bitcast(I32))
 
         def load_w(a, lo, hi):
             if a < PASSES8:
@@ -112,22 +121,25 @@ def tile_moe_tk_lin_none_kernel(
         load_x(0, 0, T)
         load_x(1, 0, T)
         load_x(4, 0, T)
+        half = E // 2
+        load_x(3, 0, T)
+        load_w(2, 0, E)
+        load_s4(0)
+        load_s4(1)
+        load_w(0, 0, half)
+        load_s4(2)
+        load_s4(3)
+        load_w(0, half, E)
+        load_s8(0)
+        load_s8(1)
+        load_w(1, 0, half)
+        load_s8(2)
+        load_s8(3)
+        load_w(1, half, E)
+        load_w(3, 0, E)
+        load_w(4, 0, E)
         for r, pos in enumerate((pos1, pos2, pos3, pos4)):
             nc.sync.dma_start(pos_lists[r][:], pos)
-        for r in range(4):
-            nc.sync.dma_start(
-                s4[r:P:32, :, :].bitcast(I32),
-                w4_scales.rearrange("e a (q r) n -> r q (e a) n", r=4)[r].bitcast(I32),
-            )
-        for a in range(PASSES8):
-            for r in range(4):
-                nc.sync.dma_start(
-                    s8[PLACE[a][1] + r : P : 32, :, :].bitcast(I32),
-                    w8_scales[:, a].rearrange("e (q r) n -> r q e n", r=4)[r].bitcast(I32),
-                )
-        load_x(3, 0, T)
-        for a in SUM_ORDER:
-            load_w(a, 0, E)
 
         make_identity(nc, ident[:])
         nc.vector.memset(planes[:].bitcast(I32), 0)
@@ -145,7 +157,7 @@ def tile_moe_tk_lin_none_kernel(
                 s = slice(C * e, C * (e + 1))
                 if a < PASSES8:
                     lhsT = w[a][:, e, 4 * P * h : 4 * P * (h + 1)].bitcast(FP8X4)
-                    lhsT_scale = s8[row:P, e, ch]
+                    lhsT_scale = s8[S8_ROW:P, PASSES8 * e + a, ch]
                 else:
                     lhsT = w[a][:, e, 2 * P * h : 2 * P * (h + 1)].bitcast(FP4X4)
                     lhsT_scale = s4[:, PASSES4 * e + a - PASSES8, ch]
@@ -177,11 +189,17 @@ def tile_moe_tk_lin_none_kernel(
         for a in ORDER[1:]:
             turn(big[a], a, 0, 256)
             turn(small[a], a, 256, T)
-        for a in (2, 0):
-            quantise(a)
-            gather_words(a, 0, SLOTS)
+        words[0] = tile([P, SLOTS], U32, "words0", tag="raw1")
+        words[1] = tile([P, SLOTS], U32, "words1", tag="raw4")
+        bytes_g[1] = tile([P, SLOTS], U8, "bytes1", tag="raw3")
+        quantise(2)
+        gather_words(2, 0, SLOTS)
+        quantise(0)
         quantise(1)
+        gather_words(0, 0, SLOTS)
         quantise(4)
+        gather_words(1, 0, SLOTS)
+        quantise(3)
         gather_bytes(1, 0, SLOTS)
         for r in range(4):
             nc.sync.dma_start(
@@ -189,15 +207,15 @@ def tile_moe_tk_lin_none_kernel(
             )
         products(2)
         products(0)
-        gather_words(1, 0, SLOTS)
         products(1)
-        quantise(3)
-        gates = tile([P, TOP, T], F32, "gates", tag="big3")
-        nc.sync.dma_start(gates[:], gate[:, 0:P, :].rearrange("r p t -> p r t"))
+        gates = tile([P, TOP - 1, T], F32, "gates", tag="words2")
+        nc.sync.dma_start(gates[:], gate[0 : TOP - 1, 0:P, :].rearrange("r p t -> p r t"))
+        last_gate = tile([P, T], F32, "last_gate", tag="raw1")
+        nc.sync.dma_start(last_gate[:], gate[TOP - 1, 0:P, :])
         gather_bytes(0, 0, SLOTS)
         gather_words(3, 0, SLOTS)
         products(3)
-        words.append(tile([P, SLOTS], U32, "words4", tag="planes"))
+        words[4] = tile([P, SLOTS], U32, "words4", tag="planes")
         for b, experts in enumerate(BANKS):
             gather_words(4, C * experts[0], C * (experts[-1] + 1))
             for h in range(HALVES):
@@ -215,23 +233,26 @@ def tile_moe_tk_lin_none_kernel(
         blocks = T // P
         back = []
         for h in range(HALVES):
-            there = psum.tile([P, 512], F32, name="bank")
+            there = [psum.tile([P, P], F32, name="bank") for b in range(blocks)]
             for r in range(TOP - 1):
                 fetch(h, r)
                 for b in range(blocks):
                     nc.tensor.matmul(
-                        there[:, P * b : P * (b + 1)],
+                        there[b][:],
                         prod[h][:, r, P * b : P * (b + 1)],
                         ident[:],
-                        start=(r == 0 and b == 0),
-                        stop=(r == TOP - 2 and b == blocks - 1),
+                        start=(r == 0),
+                        stop=(r == TOP - 2),
                         is_transpose=True,
                     )
-            nc.scalar.activation(turned[h][:], there[:, 0:T], COPY)
             back.append(psum.tile([P, 512], F32, name="bank"))
             for b in range(blocks):
-                nc.tensor.transpose(back[h][:, P * b : P * (b + 1)], turned[h][:, P * b : P * (b + 1)], ident[:])
+                cols = slice(P * b, P * (b + 1))
+                nc.scalar.activation(turned[h][:, cols], there[b][:], COPY)
+                nc.tensor.transpose(back[h][:, cols], turned[h][:, cols], ident[:])
+        last_prod = tile([P, HALVES, T], F32, "last_prod", tag="words2")
         for h in range(HALVES):
-            fetch(h, TOP - 1)
-            nc.vector.tensor_tensor(res[h][:], back[h][:, 0:T], prod[h][:, TOP - 1, :], ADD)
+            nc.vector.tensor_tensor(last_prod[:, h, :], y[h][:].indirect(pos_lists[TOP - 1][:]), last_gate[:], MULT)
+        for h in range(HALVES):
+            nc.vector.tensor_tensor(res[h][:], back[h][:, 0:T], last_prod[:, h, :], ADD)
             nc.sync.dma_start(out[P * h : P * (h + 1), :], res[h][:])

@@ -25,13 +25,13 @@ PASSES4 = 3
 HALVES = N // P
 FLOPS = 2 * SLOTS * K * N
 
-ORDER = (2, 0, 1, 4, 3)
-SUM_ORDER = (2, 0, 1, 3, 4)
+ORDER = (3, 2, 0, 1, 4)
+SUM_ORDER = ORDER
+LATE = ORDER[2:]
 WIDE = 2048
-PLACE = {2: (1, 0), 0: (1, 4), 1: (1, 8), 4: (1, 12), 3: (0, 0)}
+PLACE = {2: (0, 0), 0: (0, 4), 1: (0, 8), 4: (0, 12), 3: (1, 0)}
 PLANES = 2
 MOVED = 4
-S8_ROW = 8
 BANKS = ((0, 1, 2, 3), (4, 5, 6, 7), (8, 9, 10), (11,))
 
 
@@ -41,6 +41,7 @@ def tile_moe_tk_lin_none_kernel(
     nc = tc.nc
     with ExitStack() as ctx:
         keep = ctx.enter_context(tc.tile_pool(name="keep", bufs=1))
+        overlay = ctx.enter_context(tc.tile_pool(name="overlay", bufs=1))
         psum = ctx.enter_context(tc.psum_pool(name="psum", bufs=8))
 
         def tile(shape, dtype, name, tag=""):
@@ -53,13 +54,16 @@ def tile_moe_tk_lin_none_kernel(
         big = [tile([P, 256, 4], BF16, "big%d" % a) for a in range(PASSES)]
         small = [tile([P, 128, 4], BF16, "small%d" % a) for a in range(PASSES)]
         codes = tile([P, (PASSES - 1) * T + WIDE], U32, "codes")
-        planes = tile([P, (PLANES - 1) * T + WIDE], U8, "planes")
-        words = {a: tile([P, SLOTS], U32, "words%d" % a) for a in (2, 3)}
-        bytes_g = {0: tile([P, SLOTS], U8, "bytes0")}
+        late_bytes = 4 * SLOTS * len(LATE)
+        planes = overlay.tile(
+            [P, (PLANES - 1) * T + WIDE], U8, name="planes", align_bytes=64, offset=late_bytes - WIDE // 2
+        )
+        words = {3: tile([P, SLOTS], U32, "words3")}
+        bytes_g = [tile([P, SLOTS], U8, "bytes%d" % i) for i in range(PLANES)]
         moved = tile([P, SLOTS], U8, "moved")
         s4 = tile([P, E * PASSES4, N], U8, "s4")
-        s8 = tile([P, E * PASSES8, N], U8, "s8")
-        w = [tile([P, E, (4 if a < PASSES8 else 2) * N], U8, "w%d" % a) for a in range(PASSES)]
+        s8 = tile([P, E, N], U8, "s8")
+        w = [tile([P, E, (4 if a < PASSES8 else 2) * N], U8, "w%d" % a) for a in range(PASSES - 1)]
         y = [tile([P, SLOTS], F32, "y%d" % h) for h in range(HALVES)]
         prod = [tile([P, TOP - 1, T], F32, "prod%d" % h) for h in range(HALVES)]
         turned = [tile([P, T], F32, "turned%d" % h) for h in range(HALVES)]
@@ -77,9 +81,9 @@ def tile_moe_tk_lin_none_kernel(
             src = w4_scales.rearrange("e a (q r) n -> r q (e a) n", r=4)[r]
             nc.sync.dma_start(s4[r:P:32, :, :].bitcast(I32), src.bitcast(I32))
 
-        def load_s8(r):
-            src = w8_scales.rearrange("e a (q r) n -> r q (e a) n", r=4)[r]
-            nc.sync.dma_start(s8[S8_ROW + r : P : 32, :, :].bitcast(I32), src.bitcast(I32))
+        def load_s8(a, r):
+            src = w8_scales[:, a].rearrange("e (q r) n -> r q e n", r=4)[r]
+            nc.sync.dma_start(s8[PLACE[a][1] + r : P : 32, :, :].bitcast(I32), src.bitcast(I32))
 
         def load_w(a, lo, hi):
             if a < PASSES8:
@@ -115,31 +119,21 @@ def tile_moe_tk_lin_none_kernel(
             window = planes[:, T * i : T * i + width(hi - lo)]
             nc.vector.tensor_copy(out=bytes_g[i][:, lo:hi], in_=window.indirect(offs_list[:, lo // 16 : hi // 16]))
 
-        load_x(2, 0, 256)
-        load_x(2, 256, T)
-        nc.sync.dma_start(offs_list[:], offs)
-        load_x(0, 0, T)
-        load_x(1, 0, T)
-        load_x(4, 0, T)
-        half = E // 2
         load_x(3, 0, T)
-        load_w(2, 0, E)
-        load_s4(0)
-        load_s4(1)
-        load_w(0, 0, half)
-        load_s4(2)
-        load_s4(3)
-        load_w(0, half, E)
-        load_s8(0)
-        load_s8(1)
-        load_w(1, 0, half)
-        load_s8(2)
-        load_s8(3)
-        load_w(1, half, E)
-        load_w(3, 0, E)
-        load_w(4, 0, E)
+        nc.sync.dma_start(offs_list[:], offs)
+        for a in ORDER[1:]:
+            load_x(a, 0, T)
         for r, pos in enumerate((pos1, pos2, pos3, pos4)):
             nc.sync.dma_start(pos_lists[r][:], pos)
+        for r in range(4):
+            load_s4(r)
+        for a in range(PASSES8):
+            for r in range(4):
+                load_s8(a, r)
+        for a in ORDER[:-2]:
+            load_w(a, 0, E)
+        for lo in range(0, E, 4):
+            load_w(ORDER[-2], lo, lo + 4)
 
         make_identity(nc, ident[:])
         nc.vector.memset(planes[:].bitcast(I32), 0)
@@ -157,7 +151,7 @@ def tile_moe_tk_lin_none_kernel(
                 s = slice(C * e, C * (e + 1))
                 if a < PASSES8:
                     lhsT = w[a][:, e, 4 * P * h : 4 * P * (h + 1)].bitcast(FP8X4)
-                    lhsT_scale = s8[S8_ROW:P, PASSES8 * e + a, ch]
+                    lhsT_scale = s8[row:P, e, ch]
                 else:
                     lhsT = w[a][:, e, 2 * P * h : 2 * P * (h + 1)].bitcast(FP4X4)
                     lhsT_scale = s4[:, PASSES4 * e + a - PASSES8, ch]
@@ -184,38 +178,44 @@ def tile_moe_tk_lin_none_kernel(
             else:
                 nc.scalar.activation(dst, src, COPY)
 
-        turn(big[2], 2, 0, 256, on_vector=True)
-        turn(small[2], 2, 256, T)
+        turn(big[3], 3, 0, 256, on_vector=True)
+        turn(small[3], 3, 256, T)
         for a in ORDER[1:]:
             turn(big[a], a, 0, 256)
             turn(small[a], a, 256, T)
-        words[0] = tile([P, SLOTS], U32, "words0", tag="raw1")
-        words[1] = tile([P, SLOTS], U32, "words1", tag="raw4")
-        bytes_g[1] = tile([P, SLOTS], U8, "bytes1", tag="raw3")
-        quantise(2)
-        gather_words(2, 0, SLOTS)
-        quantise(0)
-        quantise(1)
-        gather_words(0, 0, SLOTS)
-        quantise(4)
-        gather_words(1, 0, SLOTS)
         quantise(3)
+        gather_words(3, 0, SLOTS)
         gather_bytes(1, 0, SLOTS)
+        products(3)
+        words[2] = tile([P, SLOTS], U32, "words2", tag="raw0")
+        quantise(2)
+        quantise(0)
+        gather_words(2, 0, SLOTS)
+        quantise(1)
+        quantise(4)
+        gather_bytes(0, 0, SLOTS)
         for r in range(4):
             nc.sync.dma_start(
-                moved[r:P:32, :].bitcast(I32), bytes_g[1][PLACE[MOVED][1] + r : P : 32, :].bitcast(I32)
+                moved[r:P:32, :].bitcast(I32), bytes_g[0][PLACE[MOVED][1] + r : P : 32, :].bitcast(I32)
             )
-        products(2)
-        products(0)
-        products(1)
-        gates = tile([P, TOP - 1, T], F32, "gates", tag="words2")
-        nc.sync.dma_start(gates[:], gate[0 : TOP - 1, 0:P, :].rearrange("r p t -> p r t"))
-        last_gate = tile([P, T], F32, "last_gate", tag="raw1")
+        late_words = overlay.tile([P, len(LATE), SLOTS], U32, name="late_words", align_bytes=64, offset=0)
+        for i, a in enumerate(LATE):
+            words[a] = late_words[:, i, :]
+        w.append(overlay.tile([P, E, 2 * N], U8, name="w4", align_bytes=64, offset=late_bytes))
+        for lo in range(0, E, 4):
+            load_w(4, lo, lo + 4)
+        gates = tile([P, TOP - 1, T], F32, "gates", tag="words3")
+        for r in range(TOP - 1):
+            nc.sync.dma_start(gates[:, r, :], gate[r, 0:P, :])
+        last_gate = tile([P, T], F32, "last_gate", tag="w3")
         nc.sync.dma_start(last_gate[:], gate[TOP - 1, 0:P, :])
-        gather_bytes(0, 0, SLOTS)
-        gather_words(3, 0, SLOTS)
-        products(3)
-        words[4] = tile([P, SLOTS], U32, "words4", tag="planes")
+        products(2)
+        gather_words(0, 0, SLOTS)
+        products(0)
+        cut = C * BANKS[2][0]
+        gather_words(1, 0, cut)
+        gather_words(1, cut, SLOTS)
+        products(1)
         for b, experts in enumerate(BANKS):
             gather_words(4, C * experts[0], C * (experts[-1] + 1))
             for h in range(HALVES):
@@ -250,7 +250,7 @@ def tile_moe_tk_lin_none_kernel(
                 cols = slice(P * b, P * (b + 1))
                 nc.scalar.activation(turned[h][:, cols], there[b][:], COPY)
                 nc.tensor.transpose(back[h][:, cols], turned[h][:, cols], ident[:])
-        last_prod = tile([P, HALVES, T], F32, "last_prod", tag="words2")
+        last_prod = tile([P, HALVES, T], F32, "last_prod", tag="words3")
         for h in range(HALVES):
             nc.vector.tensor_tensor(last_prod[:, h, :], y[h][:].indirect(pos_lists[TOP - 1][:]), last_gate[:], MULT)
         for h in range(HALVES):

@@ -32,7 +32,11 @@ WIDE = 2048
 PLACE = {2: (0, 0), 0: (0, 4), 1: (0, 8), 4: (0, 12), 3: (1, 0)}
 PLANES = 2
 MOVED = 4
-BANKS = ((0, 1, 2, 3), (4, 5, 6, 7), (8, 9, 10), (11,))
+BANKS = (
+    ((0, 1, 2, 3), (4, 5, 6, 7), (8, 9), (10,), (11,)),
+    ((0, 1, 2, 3), (4, 5, 6, 7), (8, 9, 10, 11)),
+)
+EARLY = 1024
 
 
 def tile_moe_tk_lin_none_kernel(
@@ -50,20 +54,24 @@ def tile_moe_tk_lin_none_kernel(
         offs_list = keep.tile([P, SLOTS // 16], U16, name="offs_list")
         pos_lists = [keep.tile([P, T // 16], U16, name="pos%d_list" % r) for r in range(TOP)]
 
-        raw = [tile([P, 4, T], F32, "raw%d" % a) for a in range(PASSES)]
-        big = [tile([P, 256, 4], BF16, "big%d" % a) for a in range(PASSES)]
-        small = [tile([P, 128, 4], BF16, "small%d" % a) for a in range(PASSES)]
+        first = [tile([P, 4, P], F32, "first%d" % c) for c in range(3)]
+        first_bf = [tile([P, P, 4], BF16, "first_bf%d" % c) for c in range(3)]
+        raw = {a: tile([P, 4, T], F32, "raw%d" % a) for a in ORDER[1:-1]}
+        raw[4] = overlay.tile([P, 4, T], F32, name="raw4", align_bytes=64, offset=0)
+        big = {a: tile([P, 256, 4], BF16, "big%d" % a) for a in ORDER[1:]}
+        small = {a: tile([P, 128, 4], BF16, "small%d" % a) for a in ORDER[1:]}
         codes = tile([P, (PASSES - 1) * T + WIDE], U32, "codes")
-        late_bytes = 4 * SLOTS * len(LATE)
-        planes = overlay.tile(
-            [P, (PLANES - 1) * T + WIDE], U8, name="planes", align_bytes=64, offset=late_bytes - WIDE // 2
-        )
+        rest_bytes = 4 * (SLOTS - EARLY)
+        late_bytes = rest_bytes + 4 * SLOTS * len(LATE)
+        planes = overlay.tile([P, (PLANES - 1) * T + WIDE], U8, name="planes", align_bytes=64, offset=late_bytes)
+        gate_bytes = late_bytes + 2 * N * E
         words = {3: tile([P, SLOTS], U32, "words3")}
         bytes_g = [tile([P, SLOTS], U8, "bytes%d" % i) for i in range(PLANES)]
         moved = tile([P, SLOTS], U8, "moved")
         s4 = tile([P, E * PASSES4, N], U8, "s4")
         s8 = tile([P, E, N], U8, "s8")
-        w = [tile([P, E, (4 if a < PASSES8 else 2) * N], U8, "w%d" % a) for a in range(PASSES - 1)]
+        w = {a: tile([P, E, (4 if a < PASSES8 else 2) * N], U8, "w%d" % a) for a in (0, 1, 3)}
+        w[2] = overlay.tile([P, E, 2 * N], U8, name="w2", align_bytes=64, offset=gate_bytes)
         y = [tile([P, SLOTS], F32, "y%d" % h) for h in range(HALVES)]
         prod = [tile([P, TOP - 1, T], F32, "prod%d" % h) for h in range(HALVES)]
         turned = [tile([P, T], F32, "turned%d" % h) for h in range(HALVES)]
@@ -75,7 +83,8 @@ def tile_moe_tk_lin_none_kernel(
 
         def load_x(a, lo, hi):
             rows = xT[512 * a : 512 * (a + 1), :].rearrange("(p j) w -> p j w", j=4)
-            nc.sync.dma_start(raw[a][:, :, lo:hi], rows[:, :, lo:hi])
+            dst = first[lo // P][:] if a == ORDER[0] else raw[a][:, :, lo:hi]
+            nc.sync.dma_start(dst, rows[:, :, lo:hi])
 
         def load_s4(r):
             src = w4_scales.rearrange("e a (q r) n -> r q (e a) n", r=4)[r]
@@ -83,7 +92,7 @@ def tile_moe_tk_lin_none_kernel(
 
         def load_s8(a, r):
             src = w8_scales[:, a].rearrange("e (q r) n -> r q e n", r=4)[r]
-            nc.sync.dma_start(s8[PLACE[a][1] + r : P : 32, :, :].bitcast(I32), src.bitcast(I32))
+            nc.gpsimd.dma_start(s8[PLACE[a][1] + r : P : 32, :, :].bitcast(I32), src.bitcast(I32))
 
         def load_w(a, lo, hi):
             if a < PASSES8:
@@ -92,34 +101,44 @@ def tile_moe_tk_lin_none_kernel(
                 src = w4_words[lo:hi, a - PASSES8].rearrange("e p b -> p e b")
             nc.sync.dma_start(w[a][:, lo:hi, :].bitcast(I32), src.bitcast(I32))
 
-        def turn(dst, a, lo, hi, on_vector=False):
-            src = raw[a][:, :, lo:hi].rearrange("p j w -> p w j")
+        def turn(dst, src, on_vector=False):
+            src = src.rearrange("p j (c i) -> p c j i", i=4)
+            dst = dst[:].rearrange("p (c i) j -> p c j i", i=4)
             if on_vector:
-                nc.vector.tensor_copy(out=dst[:], in_=src)
+                nc.vector.tensor_copy(out=dst, in_=src)
             else:
-                nc.scalar.activation(dst[:], src, COPY)
+                nc.scalar.activation(dst, src, COPY)
+
+        def quantise_part(a, src, lo, hi):
+            i, row = PLACE[a]
+            nc.vector.quantize_mx(
+                out=codes[:, home(a) + lo : home(a) + hi].bitcast(FP8X4),
+                scales=planes[row:P, T * i + lo : T * i + hi],
+                in_=src[:].rearrange("p w j -> p (w j)"),
+            )
 
         def quantise(a):
-            i, row = PLACE[a]
-            for src, lo, hi in ((big[a], 0, 256), (small[a], 256, T)):
-                nc.vector.quantize_mx(
-                    out=codes[:, home(a) + lo : home(a) + hi].bitcast(FP8X4),
-                    scales=planes[row:P, T * i + lo : T * i + hi],
-                    in_=src[:].rearrange("p w j -> p (w j)"),
-                )
+            quantise_part(a, big[a], 0, 256)
+            quantise_part(a, small[a], 256, T)
 
         def width(count):
             return 512 if count <= 384 else 1024 if count <= 768 else WIDE
 
+        def slots_of(a, lo, hi):
+            if a == 2 and lo >= EARLY:
+                return words["rest"][:, lo - EARLY : hi - EARLY]
+            return words[a][:, lo:hi]
+
         def gather_words(a, lo, hi):
             window = codes[:, home(a) : home(a) + width(hi - lo)]
-            nc.vector.tensor_copy(out=words[a][:, lo:hi], in_=window.indirect(offs_list[:, lo // 16 : hi // 16]))
+            nc.vector.tensor_copy(out=slots_of(a, lo, hi), in_=window.indirect(offs_list[:, lo // 16 : hi // 16]))
 
         def gather_bytes(i, lo, hi):
             window = planes[:, T * i : T * i + width(hi - lo)]
             nc.vector.tensor_copy(out=bytes_g[i][:, lo:hi], in_=window.indirect(offs_list[:, lo // 16 : hi // 16]))
 
-        load_x(3, 0, T)
+        for c in range(3):
+            load_x(3, P * c, P * (c + 1))
         nc.sync.dma_start(offs_list[:], offs)
         for a in ORDER[1:]:
             load_x(a, 0, T)
@@ -140,95 +159,110 @@ def tile_moe_tk_lin_none_kernel(
         nc.vector.memset(codes[:, PASSES * T :].bitcast(I32), 0)
 
         banks = {}
-        for b in range(len(BANKS)):
-            for h in range(HALVES):
-                banks[b, h] = psum.tile([P, 512], F32, name="bank")
+        home_bank = {}
+        for h in range(HALVES):
+            for b, experts in enumerate(BANKS[h]):
+                banks[h, b] = psum.tile([P, 512], F32, name="bank")
+                for e in experts:
+                    home_bank[h, e] = b
 
-        def step(b, h, a):
+        def product(e, h, a):
             ch = slice(P * h, P * (h + 1))
             i, row = PLACE[a]
-            for col, e in enumerate(BANKS[b]):
-                s = slice(C * e, C * (e + 1))
-                if a < PASSES8:
-                    lhsT = w[a][:, e, 4 * P * h : 4 * P * (h + 1)].bitcast(FP8X4)
-                    lhsT_scale = s8[row:P, e, ch]
-                else:
-                    lhsT = w[a][:, e, 2 * P * h : 2 * P * (h + 1)].bitcast(FP4X4)
-                    lhsT_scale = s4[:, PASSES4 * e + a - PASSES8, ch]
-                nc.tensor.matmul_mx(
-                    out=banks[b, h][:, C * col : C * (col + 1)],
-                    lhsT=lhsT,
-                    lhsT_scale=lhsT_scale,
-                    rhs=words[a][:, s].bitcast(FP8X4),
-                    rhs_scale=moved[:, s] if a == MOVED else bytes_g[i][row:P, s],
-                    start=(a == SUM_ORDER[0] and col == 0),
-                    stop=(a == SUM_ORDER[-1] and e == BANKS[b][-1]),
-                )
+            b = home_bank[h, e]
+            col = e - BANKS[h][b][0]
+            s = slice(C * e, C * (e + 1))
+            if a < PASSES8:
+                lhsT = w[a][:, e, 4 * P * h : 4 * P * (h + 1)].bitcast(FP8X4)
+                lhsT_scale = s8[row:P, e, ch]
+            else:
+                lhsT = w[a][:, e, 2 * P * h : 2 * P * (h + 1)].bitcast(FP4X4)
+                lhsT_scale = s4[:, PASSES4 * e + a - PASSES8, ch]
+            nc.tensor.matmul_mx(
+                out=banks[h, b][:, C * col : C * (col + 1)],
+                lhsT=lhsT,
+                lhsT_scale=lhsT_scale,
+                rhs=slots_of(a, C * e, C * (e + 1)).bitcast(FP8X4),
+                rhs_scale=moved[:, s] if a == MOVED else bytes_g[i][row:P, s],
+                start=(a == SUM_ORDER[0] and col == 0),
+                stop=(a == SUM_ORDER[-1] and e == BANKS[h][b][-1]),
+            )
 
         def products(a):
-            for b in range(len(BANKS)):
+            for lo in range(0, E, 4):
                 for h in range(HALVES):
-                    step(b, h, a)
+                    for e in range(lo, lo + 4):
+                        product(e, h, a)
 
-        def empty(b, h, on_vector=False):
-            dst = y[h][:, C * BANKS[b][0] : C * (BANKS[b][-1] + 1)]
-            src = banks[b, h][:, 0 : C * len(BANKS[b])]
+        def empty(h, b, on_vector=False):
+            experts = BANKS[h][b]
+            dst = y[h][:, C * experts[0] : C * (experts[-1] + 1)]
+            src = banks[h, b][:, 0 : C * len(experts)]
             if on_vector:
                 nc.vector.tensor_copy(out=dst, in_=src)
             else:
                 nc.scalar.activation(dst, src, COPY)
 
-        turn(big[3], 3, 0, 256, on_vector=True)
-        turn(small[3], 3, 256, T)
+        turn(first_bf[0], first[0][:])
+        turn(first_bf[1], first[1][:], on_vector=True)
+        quantise_part(3, first_bf[0], 0, P)
+        turn(first_bf[2], first[2][:], on_vector=True)
+        quantise_part(3, first_bf[1], P, 2 * P)
+        quantise_part(3, first_bf[2], 2 * P, T)
         for a in ORDER[1:]:
-            turn(big[a], a, 0, 256)
-            turn(small[a], a, 256, T)
-        quantise(3)
+            turn(big[a], raw[a][:, :, 0:256])
+            turn(small[a], raw[a][:, :, 256:T])
         gather_words(3, 0, SLOTS)
         gather_bytes(1, 0, SLOTS)
         products(3)
-        words[2] = tile([P, SLOTS], U32, "words2", tag="raw0")
+        words[2] = tile([P, EARLY], U32, "words2", tag="raw0")
         quantise(2)
         quantise(0)
-        gather_words(2, 0, SLOTS)
+        gather_words(2, 0, EARLY)
         quantise(1)
         quantise(4)
+        words["rest"] = overlay.tile([P, SLOTS - EARLY], U32, name="rest", align_bytes=64, offset=0)
+        gather_words(2, EARLY, SLOTS)
         gather_bytes(0, 0, SLOTS)
         for r in range(4):
             nc.sync.dma_start(
                 moved[r:P:32, :].bitcast(I32), bytes_g[0][PLACE[MOVED][1] + r : P : 32, :].bitcast(I32)
             )
-        late_words = overlay.tile([P, len(LATE), SLOTS], U32, name="late_words", align_bytes=64, offset=0)
+        late_words = overlay.tile([P, len(LATE), SLOTS], U32, name="late_words", align_bytes=64, offset=rest_bytes)
         for i, a in enumerate(LATE):
             words[a] = late_words[:, i, :]
-        w.append(overlay.tile([P, E, 2 * N], U8, name="w4", align_bytes=64, offset=late_bytes))
+        w[4] = overlay.tile([P, E, 2 * N], U8, name="w4", align_bytes=64, offset=late_bytes)
         for lo in range(0, E, 4):
             load_w(4, lo, lo + 4)
-        gates = tile([P, TOP - 1, T], F32, "gates", tag="words3")
-        for r in range(TOP - 1):
-            nc.sync.dma_start(gates[:, r, :], gate[r, 0:P, :])
-        last_gate = tile([P, T], F32, "last_gate", tag="w3")
-        nc.sync.dma_start(last_gate[:], gate[TOP - 1, 0:P, :])
         products(2)
+        gates = []
+        for r in range(TOP):
+            g = overlay.tile([P, T], F32, name="gate%d" % r, align_bytes=64, offset=gate_bytes + 4 * T * r)
+            nc.sync.dma_start(g[:], gate[r, 0:P, :])
+            gates.append(g)
         gather_words(0, 0, SLOTS)
         products(0)
-        cut = C * BANKS[2][0]
-        gather_words(1, 0, cut)
-        gather_words(1, cut, SLOTS)
+        gather_words(1, 0, EARLY)
+        gather_words(1, EARLY, SLOTS)
         products(1)
-        for b, experts in enumerate(BANKS):
+        for experts in BANKS[0]:
             gather_words(4, C * experts[0], C * (experts[-1] + 1))
-            for h in range(HALVES):
-                step(b, h, 4)
-        last = len(BANKS) - 1
+            for e in experts:
+                product(e, 0, 4)
+            if len(experts) == 4:
+                for e in experts:
+                    product(e, 1, 4)
+        for e in BANKS[1][-1]:
+            product(e, 1, 4)
+        last = len(BANKS[0]) - 1
         for b in range(last):
-            empty(b, 0)
-        empty(last, 0, on_vector=True)
-        for b in range(len(BANKS)):
-            empty(b, 1)
+            empty(0, b)
+        empty(0, last, on_vector=True)
+        for b in range(len(BANKS[1])):
+            empty(1, b)
 
         def fetch(h, r):
-            nc.vector.tensor_tensor(prod[h][:, r, :], y[h][:].indirect(pos_lists[r][:]), gates[:, r, :], MULT)
+            nc.vector.tensor_tensor(prod[h][:, r, :], y[h][:].indirect(pos_lists[r][:]), gates[r][:], MULT)
 
         blocks = T // P
         back = []
@@ -250,9 +284,19 @@ def tile_moe_tk_lin_none_kernel(
                 cols = slice(P * b, P * (b + 1))
                 nc.scalar.activation(turned[h][:, cols], there[b][:], COPY)
                 nc.tensor.transpose(back[h][:, cols], turned[h][:, cols], ident[:])
-        last_prod = tile([P, HALVES, T], F32, "last_prod", tag="words3")
-        for h in range(HALVES):
-            nc.vector.tensor_tensor(last_prod[:, h, :], y[h][:].indirect(pos_lists[TOP - 1][:]), last_gate[:], MULT)
-        for h in range(HALVES):
-            nc.vector.tensor_tensor(res[h][:], back[h][:, 0:T], last_prod[:, h, :], ADD)
-            nc.sync.dma_start(out[P * h : P * (h + 1), :], res[h][:])
+        last_prod = overlay.tile([P, HALVES, T], F32, name="last_prod", align_bytes=64, offset=gate_bytes)
+
+        def fetch_last(h, lo, hi):
+            window = y[h][:].indirect(pos_lists[TOP - 1][:, lo // 16 : hi // 16])
+            nc.vector.tensor_tensor(last_prod[:, h, lo:hi], window, gates[TOP - 1][:, lo:hi], MULT)
+
+        def finish(h, lo, hi):
+            nc.vector.tensor_tensor(res[h][:, lo:hi], back[h][:, lo:hi], last_prod[:, h, lo:hi], ADD)
+            nc.sync.dma_start(out[P * h : P * (h + 1), lo:hi], res[h][:, lo:hi])
+
+        fetch_last(0, 0, T)
+        fetch_last(1, 0, 256)
+        finish(0, 0, T)
+        fetch_last(1, 256, T)
+        finish(1, 0, 256)
+        finish(1, 256, T)

@@ -26,12 +26,13 @@ HALVES = N // P
 FLOPS = 2 * SLOTS * K * N
 
 ORDER = (3, 2, 0, 1, 4)
-SUM_ORDER = ORDER
+SUM_ORDER = (2, 0, 1, 3, 4)
 LATE = ORDER[2:]
 WIDE = 2048
 PLACE = {2: (0, 0), 0: (0, 4), 1: (0, 8), 4: (0, 12), 3: (1, 0)}
 PLANES = 2
-MOVED = 4
+FIFTH = 16
+MOVED = {3: FIFTH, 4: 12}
 BANKS = (
     ((0, 1, 2, 3), (4, 5, 6, 7), (8, 9), (10,), (11,)),
     ((0, 1, 2, 3), (4, 5, 6, 7), (8, 9, 10, 11)),
@@ -46,6 +47,7 @@ def tile_moe_tk_lin_none_kernel(
     with ExitStack() as ctx:
         keep = ctx.enter_context(tc.tile_pool(name="keep", bufs=1))
         overlay = ctx.enter_context(tc.tile_pool(name="overlay", bufs=1))
+        held = ctx.enter_context(tc.tile_pool(name="held", bufs=1))
         psum = ctx.enter_context(tc.psum_pool(name="psum", bufs=8))
 
         def tile(shape, dtype, name, tag=""):
@@ -55,23 +57,21 @@ def tile_moe_tk_lin_none_kernel(
         pos_lists = [keep.tile([P, T // 16], U16, name="pos%d_list" % r) for r in range(TOP)]
 
         first = [tile([P, 4, P], F32, "first%d" % c) for c in range(3)]
-        first_bf = [tile([P, P, 4], BF16, "first_bf%d" % c) for c in range(3)]
-        raw = {a: tile([P, 4, T], F32, "raw%d" % a) for a in ORDER[1:-1]}
-        raw[4] = overlay.tile([P, 4, T], F32, name="raw4", align_bytes=64, offset=0)
+        first_bf = [tile([P, P, 4], BF16, "first_bf%d" % c) for c in range(2)]
+        s4_bytes = E * PASSES4 * N
+        first_bf.append(held.tile([P, P, 4], BF16, name="first_bf2", align_bytes=64, offset=s4_bytes - 512))
+        raw = {a: tile([P, 4, T], F32, "raw%d" % a) for a in ORDER[1:]}
         big = {a: tile([P, 256, 4], BF16, "big%d" % a) for a in ORDER[1:]}
         small = {a: tile([P, 128, 4], BF16, "small%d" % a) for a in ORDER[1:]}
         codes = tile([P, (PASSES - 1) * T + WIDE], U32, "codes")
-        rest_bytes = 4 * (SLOTS - EARLY)
-        late_bytes = rest_bytes + 4 * SLOTS * len(LATE)
-        planes = overlay.tile([P, (PLANES - 1) * T + WIDE], U8, name="planes", align_bytes=64, offset=late_bytes)
-        gate_bytes = late_bytes + 2 * N * E
+        planes = tile([P, PLANES * T], U8, "planes")
+        weight_bytes = 2 * N * E
+        packed = overlay.tile([P, WIDE], U8, name="packed", align_bytes=64, offset=weight_bytes - WIDE // 2)
         words = {3: tile([P, SLOTS], U32, "words3")}
-        bytes_g = [tile([P, SLOTS], U8, "bytes%d" % i) for i in range(PLANES)]
-        moved = tile([P, SLOTS], U8, "moved")
-        s4 = tile([P, E * PASSES4, N], U8, "s4")
+        bytes_g = tile([P, SLOTS], U8, "bytes_g")
+        moved = {a: tile([P, SLOTS], U8, "moved%d" % a) for a in MOVED}
         s8 = tile([P, E, N], U8, "s8")
-        w = {a: tile([P, E, (4 if a < PASSES8 else 2) * N], U8, "w%d" % a) for a in (0, 1, 3)}
-        w[2] = overlay.tile([P, E, 2 * N], U8, name="w2", align_bytes=64, offset=gate_bytes)
+        w = {}
         y = [tile([P, SLOTS], F32, "y%d" % h) for h in range(HALVES)]
         prod = [tile([P, TOP - 1, T], F32, "prod%d" % h) for h in range(HALVES)]
         turned = [tile([P, T], F32, "turned%d" % h) for h in range(HALVES)]
@@ -125,17 +125,15 @@ def tile_moe_tk_lin_none_kernel(
             return 512 if count <= 384 else 1024 if count <= 768 else WIDE
 
         def slots_of(a, lo, hi):
-            if a == 2 and lo >= EARLY:
-                return words["rest"][:, lo - EARLY : hi - EARLY]
             return words[a][:, lo:hi]
 
         def gather_words(a, lo, hi):
             window = codes[:, home(a) : home(a) + width(hi - lo)]
             nc.vector.tensor_copy(out=slots_of(a, lo, hi), in_=window.indirect(offs_list[:, lo // 16 : hi // 16]))
 
-        def gather_bytes(i, lo, hi):
-            window = planes[:, T * i : T * i + width(hi - lo)]
-            nc.vector.tensor_copy(out=bytes_g[i][:, lo:hi], in_=window.indirect(offs_list[:, lo // 16 : hi // 16]))
+        def move(a):
+            for r in range(4):
+                nc.sync.dma_start(moved[a][r:P:32, :].bitcast(I32), bytes_g[MOVED[a] + r : P : 32, :].bitcast(I32))
 
         for c in range(3):
             load_x(3, P * c, P * (c + 1))
@@ -144,18 +142,13 @@ def tile_moe_tk_lin_none_kernel(
             load_x(a, 0, T)
         for r, pos in enumerate((pos1, pos2, pos3, pos4)):
             nc.sync.dma_start(pos_lists[r][:], pos)
-        for r in range(4):
-            load_s4(r)
         for a in range(PASSES8):
             for r in range(4):
                 load_s8(a, r)
-        for a in ORDER[:-2]:
-            load_w(a, 0, E)
-        for lo in range(0, E, 4):
-            load_w(ORDER[-2], lo, lo + 4)
 
         make_identity(nc, ident[:])
         nc.vector.memset(planes[:].bitcast(I32), 0)
+        nc.vector.memset(packed[:].bitcast(I32), 0)
         nc.vector.memset(codes[:, PASSES * T :].bitcast(I32), 0)
 
         banks = {}
@@ -183,7 +176,7 @@ def tile_moe_tk_lin_none_kernel(
                 lhsT=lhsT,
                 lhsT_scale=lhsT_scale,
                 rhs=slots_of(a, C * e, C * (e + 1)).bitcast(FP8X4),
-                rhs_scale=moved[:, s] if a == MOVED else bytes_g[i][row:P, s],
+                rhs_scale=moved[a][:, s] if a in MOVED else bytes_g[row:P, s],
                 start=(a == SUM_ORDER[0] and col == 0),
                 stop=(a == SUM_ORDER[-1] and e == BANKS[h][b][-1]),
             )
@@ -209,35 +202,45 @@ def tile_moe_tk_lin_none_kernel(
         turn(first_bf[2], first[2][:], on_vector=True)
         quantise_part(3, first_bf[1], P, 2 * P)
         quantise_part(3, first_bf[2], 2 * P, T)
+        nc.sync.dma_start(packed[FIFTH:P, 0:T].bitcast(I32), planes[0 : P - FIFTH, T : 2 * T].bitcast(I32))
+        s4 = held.tile([P, E * PASSES4, N], U8, name="s4", align_bytes=64, offset=0)
+        for r in range(4):
+            load_s4(r)
+        w[2] = held.tile([P, E, 2 * N], U8, name="w2", align_bytes=64, offset=s4_bytes)
+        load_w(2, 0, E)
         for a in ORDER[1:]:
             turn(big[a], raw[a][:, :, 0:256])
             turn(small[a], raw[a][:, :, 256:T])
+        w[0] = tile([P, E, 4 * N], U8, "w0", tag="raw2")
+        load_w(0, 0, E)
+        w[1] = tile([P, E, 4 * N], U8, "w1", tag="raw0")
+        load_w(1, 0, E)
         gather_words(3, 0, SLOTS)
-        gather_bytes(1, 0, SLOTS)
-        products(3)
-        words[2] = tile([P, EARLY], U32, "words2", tag="raw0")
+        words[2] = tile([P, SLOTS], U32, "words2", tag="big0")
         quantise(2)
         quantise(0)
-        gather_words(2, 0, EARLY)
+        gather_words(2, 0, SLOTS)
         quantise(1)
         quantise(4)
-        words["rest"] = overlay.tile([P, SLOTS - EARLY], U32, name="rest", align_bytes=64, offset=0)
-        gather_words(2, EARLY, SLOTS)
-        gather_bytes(0, 0, SLOTS)
-        for r in range(4):
-            nc.sync.dma_start(
-                moved[r:P:32, :].bitcast(I32), bytes_g[0][PLACE[MOVED][1] + r : P : 32, :].bitcast(I32)
-            )
-        late_words = overlay.tile([P, len(LATE), SLOTS], U32, name="late_words", align_bytes=64, offset=rest_bytes)
-        for i, a in enumerate(LATE):
-            words[a] = late_words[:, i, :]
-        w[4] = overlay.tile([P, E, 2 * N], U8, name="w4", align_bytes=64, offset=late_bytes)
+        for q in range(0, P, 32):
+            nc.vector.tensor_copy(out=packed[q : q + FIFTH, 0:T].bitcast(I32), in_=planes[q : q + FIFTH, 0:T].bitcast(I32))
+        nc.vector.tensor_copy(out=bytes_g[:], in_=packed[:].indirect(offs_list[:]))
+        move(3)
+        w[3] = overlay.tile([P, E, 2 * N], U8, name="w3", align_bytes=64, offset=0)
+        for lo in range(0, E, 4):
+            load_w(3, lo, lo + 4)
+        move(4)
+        w[4] = overlay.tile([P, E, 2 * N], U8, name="w4", align_bytes=64, offset=weight_bytes)
         for lo in range(0, E, 4):
             load_w(4, lo, lo + 4)
+        late_words = tile([P, len(LATE), SLOTS], U32, "late_words", tag="planes")
+        for i, a in enumerate(LATE):
+            words[a] = late_words[:, i, :]
         products(2)
+        gate_bytes = s4_bytes
         gates = []
         for r in range(TOP):
-            g = overlay.tile([P, T], F32, name="gate%d" % r, align_bytes=64, offset=gate_bytes + 4 * T * r)
+            g = held.tile([P, T], F32, name="gate%d" % r, align_bytes=64, offset=gate_bytes + 4 * T * r)
             nc.sync.dma_start(g[:], gate[r, 0:P, :])
             gates.append(g)
         gather_words(0, 0, SLOTS)
@@ -245,6 +248,7 @@ def tile_moe_tk_lin_none_kernel(
         gather_words(1, 0, EARLY)
         gather_words(1, EARLY, SLOTS)
         products(1)
+        products(3)
         for experts in BANKS[0]:
             gather_words(4, C * experts[0], C * (experts[-1] + 1))
             for e in experts:
@@ -284,7 +288,7 @@ def tile_moe_tk_lin_none_kernel(
                 cols = slice(P * b, P * (b + 1))
                 nc.scalar.activation(turned[h][:, cols], there[b][:], COPY)
                 nc.tensor.transpose(back[h][:, cols], turned[h][:, cols], ident[:])
-        last_prod = overlay.tile([P, HALVES, T], F32, name="last_prod", align_bytes=64, offset=gate_bytes)
+        last_prod = held.tile([P, HALVES, T], F32, name="last_prod", align_bytes=64, offset=gate_bytes)
 
         def fetch_last(h, lo, hi):
             window = y[h][:].indirect(pos_lists[TOP - 1][:, lo // 16 : hi // 16])

@@ -26,7 +26,7 @@ HALVES = N // P
 FLOPS = 2 * SLOTS * K * N
 
 ORDER = (3, 2, 0, 1, 4)
-SUM_ORDER = (2, 0, 1, 3, 4)
+SUM_ORDER = (2, 3, 4, 0, 1)
 LATE = ORDER[2:]
 WIDE = 2048
 PLACE = {2: (0, 0), 0: (0, 4), 1: (0, 8), 4: (0, 12), 3: (1, 0)}
@@ -48,7 +48,8 @@ def tile_moe_tk_lin_none_kernel(
         keep = ctx.enter_context(tc.tile_pool(name="keep", bufs=1))
         overlay = ctx.enter_context(tc.tile_pool(name="overlay", bufs=1))
         held = ctx.enter_context(tc.tile_pool(name="held", bufs=1))
-        psum = ctx.enter_context(tc.psum_pool(name="psum", bufs=8))
+        spread = ctx.enter_context(tc.tile_pool(name="spread", bufs=1))
+        psum = ctx.enter_context(tc.psum_pool(name="psum", bufs=1))
 
         def tile(shape, dtype, name, tag=""):
             return keep.tile(shape, dtype, name=name, tag=tag or name, align_bytes=64)
@@ -60,20 +61,22 @@ def tile_moe_tk_lin_none_kernel(
         first_bf = [tile([P, P, 4], BF16, "first_bf%d" % c) for c in range(2)]
         s4_bytes = E * PASSES4 * N
         first_bf.append(held.tile([P, P, 4], BF16, name="first_bf2", align_bytes=64, offset=s4_bytes - 512))
-        raw = {a: tile([P, 4, T], F32, "raw%d" % a) for a in ORDER[1:]}
+        raw = {a: tile([P, 4, T], F32, "raw%d" % a) for a in ORDER[1:-1]}
+        raw[4] = spread.tile([P, 4, T], F32, name="raw4", align_bytes=64, offset=0)
+        gate_rows = tile([P, T], F32, "gate_rows")
+
         big = {a: tile([P, 256, 4], BF16, "big%d" % a) for a in ORDER[1:]}
         small = {a: tile([P, 128, 4], BF16, "small%d" % a) for a in ORDER[1:]}
         codes = tile([P, (PASSES - 1) * T + WIDE], U32, "codes")
         planes = tile([P, PLANES * T], U8, "planes")
         weight_bytes = 2 * N * E
-        packed = overlay.tile([P, WIDE], U8, name="packed", align_bytes=64, offset=weight_bytes - WIDE // 2)
+        packed = overlay.tile([P, WIDE], U8, name="packed", align_bytes=64, offset=0)
         words = {3: tile([P, SLOTS], U32, "words3")}
         bytes_g = tile([P, SLOTS], U8, "bytes_g")
         moved = {a: tile([P, SLOTS], U8, "moved%d" % a) for a in MOVED}
-        s8 = tile([P, E, N], U8, "s8")
         w = {}
         y = [tile([P, SLOTS], F32, "y%d" % h) for h in range(HALVES)]
-        prod = [tile([P, TOP - 1, T], F32, "prod%d" % h) for h in range(HALVES)]
+        prod = [[tile([P, T], F32, "prod%d_%d" % (h, r)) for r in range(TOP)] for h in range(HALVES)]
         turned = [tile([P, T], F32, "turned%d" % h) for h in range(HALVES)]
         ident = tile([P, P], F32, "ident")
         res = [tile([P, T], F32, "res%d" % h) for h in range(HALVES)]
@@ -95,11 +98,12 @@ def tile_moe_tk_lin_none_kernel(
             nc.gpsimd.dma_start(s8[PLACE[a][1] + r : P : 32, :, :].bitcast(I32), src.bitcast(I32))
 
         def load_w(a, lo, hi):
-            if a < PASSES8:
-                src = w8_words[lo:hi, a].rearrange("e p n r -> p e (n r)")
-            else:
-                src = w4_words[lo:hi, a - PASSES8].rearrange("e p b -> p e b")
+            src = w4_words[lo:hi, a - PASSES8].rearrange("e p b -> p e b")
             nc.sync.dma_start(w[a][:, lo:hi, :].bitcast(I32), src.bitcast(I32))
+
+        def load_w8(a, h, lo, hi):
+            src = w8_words[lo:hi, a, :, P * h : P * (h + 1), :].rearrange("e p n r -> p e (n r)")
+            nc.sync.dma_start(w[a, h][:, lo:hi, :].bitcast(I32), src.bitcast(I32))
 
         def turn(dst, src, on_vector=False):
             src = src.rearrange("p j (c i) -> p c j i", i=4)
@@ -142,22 +146,23 @@ def tile_moe_tk_lin_none_kernel(
             load_x(a, 0, T)
         for r, pos in enumerate((pos1, pos2, pos3, pos4)):
             nc.sync.dma_start(pos_lists[r][:], pos)
-        for a in range(PASSES8):
-            for r in range(4):
-                load_s8(a, r)
-
+        nc.vector.memset(gate_rows[:], 0.0)
+        nc.sync.dma_start(gate_rows[0:TOP, :], gate[:, 0, :])
         make_identity(nc, ident[:])
         nc.vector.memset(planes[:].bitcast(I32), 0)
         nc.vector.memset(packed[:].bitcast(I32), 0)
         nc.vector.memset(codes[:, PASSES * T :].bitcast(I32), 0)
 
+        def bank(index, shape, name):
+            return psum.tile(shape, F32, name=name, tag="bank%d" % index)
+
+        by_token = bank(0, [P, T // P, P], "by_token")
+        for b in range(T // P):
+            nc.tensor.transpose(by_token[:, b, :], gate_rows[:, P * b : P * (b + 1)], ident[:])
+        wide = [bank(1 + r, [P, T], "wide%d" % r) for r in range(TOP)]
+
         banks = {}
-        home_bank = {}
-        for h in range(HALVES):
-            for b, experts in enumerate(BANKS[h]):
-                banks[h, b] = psum.tile([P, 512], F32, name="bank")
-                for e in experts:
-                    home_bank[h, e] = b
+        home_bank = {(h, e): b for h in range(HALVES) for b, experts in enumerate(BANKS[h]) for e in experts}
 
         def product(e, h, a):
             ch = slice(P * h, P * (h + 1))
@@ -166,7 +171,7 @@ def tile_moe_tk_lin_none_kernel(
             col = e - BANKS[h][b][0]
             s = slice(C * e, C * (e + 1))
             if a < PASSES8:
-                lhsT = w[a][:, e, 4 * P * h : 4 * P * (h + 1)].bitcast(FP8X4)
+                lhsT = w[a, h][:, e, :].bitcast(FP8X4)
                 lhsT_scale = s8[row:P, e, ch]
             else:
                 lhsT = w[a][:, e, 2 * P * h : 2 * P * (h + 1)].bitcast(FP4X4)
@@ -176,7 +181,7 @@ def tile_moe_tk_lin_none_kernel(
                 lhsT=lhsT,
                 lhsT_scale=lhsT_scale,
                 rhs=slots_of(a, C * e, C * (e + 1)).bitcast(FP8X4),
-                rhs_scale=moved[a][:, s] if a in MOVED else bytes_g[row:P, s],
+                rhs_scale=moved[a][:, s] if a in MOVED else scale_bytes[h, a][row:P, s],
                 start=(a == SUM_ORDER[0] and col == 0),
                 stop=(a == SUM_ORDER[-1] and e == BANKS[h][b][-1]),
             )
@@ -197,6 +202,10 @@ def tile_moe_tk_lin_none_kernel(
                 nc.scalar.activation(dst, src, COPY)
 
         turn(first_bf[0], first[0][:])
+        s8 = tile([P, E, N], U8, "s8", tag="first0")
+        for a in range(PASSES8):
+            for r in range(4):
+                load_s8(a, r)
         turn(first_bf[1], first[1][:], on_vector=True)
         quantise_part(3, first_bf[0], 0, P)
         turn(first_bf[2], first[2][:], on_vector=True)
@@ -211,10 +220,18 @@ def tile_moe_tk_lin_none_kernel(
         for a in ORDER[1:]:
             turn(big[a], raw[a][:, :, 0:256])
             turn(small[a], raw[a][:, :, 256:T])
-        w[0] = tile([P, E, 4 * N], U8, "w0", tag="raw2")
-        load_w(0, 0, E)
-        w[1] = tile([P, E, 4 * N], U8, "w1", tag="raw0")
-        load_w(1, 0, E)
+        gate_cols = spread.tile([P, T // P, TOP], F32, name="gate_cols", align_bytes=64, offset=0)
+        nc.scalar.activation(gate_cols[:], by_token[:, :, 0:TOP], COPY)
+        gates = []
+        for r in range(TOP):
+            for b in range(T // P):
+                column = gate_cols[:, b, r : r + 1].to_broadcast([P, P])
+                nc.tensor.transpose(wide[r][:, P * b : P * (b + 1)], column, ident[:])
+            g = spread.tile([P, T], F32, name="gate%d" % r, align_bytes=64, offset=64 + 4 * T * r)
+            nc.scalar.activation(g[:], wide[r][:], COPY)
+            gates.append(g)
+        w[3] = tile([P, E, 2 * N], U8, "w3", tag="raw2")
+        load_w(3, 0, E)
         gather_words(3, 0, SLOTS)
         words[2] = tile([P, SLOTS], U32, "words2", tag="big0")
         quantise(2)
@@ -225,82 +242,90 @@ def tile_moe_tk_lin_none_kernel(
         for q in range(0, P, 32):
             nc.vector.tensor_copy(out=packed[q : q + FIFTH, 0:T].bitcast(I32), in_=planes[q : q + FIFTH, 0:T].bitcast(I32))
         nc.vector.tensor_copy(out=bytes_g[:], in_=packed[:].indirect(offs_list[:]))
+        scale_bytes = {(0, 0): bytes_g, (0, 1): bytes_g, (0, 2): bytes_g, (1, 2): bytes_g}
         move(3)
-        w[3] = overlay.tile([P, E, 2 * N], U8, name="w3", align_bytes=64, offset=0)
-        for lo in range(0, E, 4):
-            load_w(3, lo, lo + 4)
+        w[4] = overlay.tile([P, E, 2 * N], U8, name="w4", align_bytes=64, offset=0)
+        load_w(4, 0, E)
         move(4)
-        w[4] = overlay.tile([P, E, 2 * N], U8, name="w4", align_bytes=64, offset=weight_bytes)
-        for lo in range(0, E, 4):
-            load_w(4, lo, lo + 4)
         late_words = tile([P, len(LATE), SLOTS], U32, "late_words", tag="planes")
         for i, a in enumerate(LATE):
             words[a] = late_words[:, i, :]
+        for h, places in enumerate(((5, 6, 7, 0, 1), (2, 3, 4))):
+            for b, place in enumerate(places):
+                banks[h, b] = bank(place, [P, 512], "sums%d_%d" % (h, b))
         products(2)
-        gate_bytes = s4_bytes
-        gates = []
-        for r in range(TOP):
-            g = held.tile([P, T], F32, name="gate%d" % r, align_bytes=64, offset=gate_bytes + 4 * T * r)
-            nc.sync.dma_start(g[:], gate[r, 0:P, :])
-            gates.append(g)
-        gather_words(0, 0, SLOTS)
-        products(0)
-        gather_words(1, 0, EARLY)
-        gather_words(1, EARLY, SLOTS)
-        products(1)
+        w[0, 0] = tile([P, E, 2 * N], U8, "w00", tag="big0")
+        load_w8(0, 0, 0, E)
+        w[1, 0] = held.tile([P, E, 2 * N], U8, name="w10", align_bytes=64, offset=s4_bytes)
+        for lo in range(0, E, 4):
+            load_w8(1, 0, lo, lo + 4)
         products(3)
+        w[0, 1] = tile([P, E, 2 * N], U8, "w01", tag="words3")
+        load_w8(0, 1, 0, E)
+        w[1, 1] = tile([P, E, 2 * N], U8, "w11", tag="raw2")
+        for lo in range(0, E, 4):
+            load_w8(1, 1, lo, lo + 4)
+        gather_words(4, 0, SLOTS)
+        products(4)
+        gather_words(0, 0, EARLY)
+        gather_words(0, EARLY, SLOTS)
+        for e in range(E):
+            product(e, 0, 0)
         for experts in BANKS[0]:
-            gather_words(4, C * experts[0], C * (experts[-1] + 1))
+            gather_words(1, C * experts[0], C * (experts[-1] + 1))
             for e in experts:
-                product(e, 0, 4)
-            if len(experts) == 4:
-                for e in experts:
-                    product(e, 1, 4)
-        for e in BANKS[1][-1]:
-            product(e, 1, 4)
+                product(e, 0, 1)
+        again = tile([P, SLOTS], U8, "again", tag="codes")
+        nc.vector.tensor_copy(out=again[:].bitcast(I32), in_=bytes_g[:].bitcast(I32))
+        scale_bytes[1, 0] = again
+        scale_bytes[1, 1] = again
         last = len(BANKS[0]) - 1
         for b in range(last):
             empty(0, b)
         empty(0, last, on_vector=True)
-        for b in range(len(BANKS[1])):
+        for b, experts in enumerate(BANKS[1]):
+            for a in range(PASSES8):
+                for e in experts:
+                    product(e, 1, a)
             empty(1, b)
 
-        def fetch(h, r):
-            nc.vector.tensor_tensor(prod[h][:, r, :], y[h][:].indirect(pos_lists[r][:]), gates[r][:], MULT)
+        def fetch(h, r, lo=0, hi=T):
+            window = y[h][:].indirect(pos_lists[r][:, lo // 16 : hi // 16])
+            nc.vector.tensor_tensor(prod[h][r][:, lo:hi], window, gates[r][:, lo:hi], MULT)
 
-        blocks = T // P
-        back = []
-        for h in range(HALVES):
-            there = [psum.tile([P, P], F32, name="bank") for b in range(blocks)]
-            for r in range(TOP - 1):
-                fetch(h, r)
-                for b in range(blocks):
-                    nc.tensor.matmul(
-                        there[b][:],
-                        prod[h][:, r, P * b : P * (b + 1)],
-                        ident[:],
-                        start=(r == 0),
-                        stop=(r == TOP - 2),
-                        is_transpose=True,
-                    )
-            back.append(psum.tile([P, 512], F32, name="bank"))
-            for b in range(blocks):
-                cols = slice(P * b, P * (b + 1))
-                nc.scalar.activation(turned[h][:, cols], there[b][:], COPY)
-                nc.tensor.transpose(back[h][:, cols], turned[h][:, cols], ident[:])
-        last_prod = held.tile([P, HALVES, T], F32, name="last_prod", align_bytes=64, offset=gate_bytes)
+        blocks = [slice(P * b, P * (b + 1)) for b in range(T // P)]
 
-        def fetch_last(h, lo, hi):
-            window = y[h][:].indirect(pos_lists[TOP - 1][:, lo // 16 : hi // 16])
-            nc.vector.tensor_tensor(last_prod[:, h, lo:hi], window, gates[TOP - 1][:, lo:hi], MULT)
+        def add_turned(dst, src, start, stop):
+            nc.tensor.matmul(dst, src, ident[:], start=start, stop=stop, is_transpose=True)
 
-        def finish(h, lo, hi):
-            nc.vector.tensor_tensor(res[h][:, lo:hi], back[h][:, lo:hi], last_prod[:, h, lo:hi], ADD)
-            nc.sync.dma_start(out[P * h : P * (h + 1), lo:hi], res[h][:, lo:hi])
-
-        fetch_last(0, 0, T)
-        fetch_last(1, 0, 256)
-        finish(0, 0, T)
-        fetch_last(1, 256, T)
-        finish(1, 0, 256)
-        finish(1, 256, T)
+        there = bank(4, [P, T], "there0")
+        for r in range(TOP):
+            fetch(0, r)
+            for cols in blocks:
+                first_one = r == 0 and cols == blocks[0]
+                last_one = r == TOP - 1 and cols == blocks[-1]
+                add_turned(there[:, cols], prod[0][r][:, cols], first_one, last_one)
+        nc.scalar.activation(turned[0][:], there[:], COPY)
+        back = [bank(5, [P, T], "back0"), bank(1, [P, T], "back1")]
+        for cols in blocks:
+            nc.tensor.transpose(back[0][:, cols], turned[0][:, cols], ident[:])
+        nc.scalar.activation(res[0][:], back[0][:], COPY)
+        nc.sync.dma_start(out[0:P, :], res[0][:])
+        parts = [bank(place, [P, P], "there1_%d" % place) for place in (6, 7, 0)]
+        for r in range(2):
+            fetch(1, r)
+            for part, cols in zip(parts, blocks):
+                add_turned(part[:], prod[1][r][:, cols], r == 0, r == 1)
+        for part, cols in zip(parts, blocks):
+            nc.scalar.activation(turned[1][:, cols], part[:], COPY)
+            nc.tensor.transpose(back[1][:, cols], turned[1][:, cols], ident[:])
+        fetch(1, 2)
+        pieces = ((0, 256), (256, T))
+        pair = tile([P, T], F32, "pair")
+        for lo, hi in pieces:
+            fetch(1, 3, lo, hi)
+        for lo, hi in pieces:
+            nc.vector.tensor_tensor(pair[:, lo:hi], prod[1][2][:, lo:hi], prod[1][3][:, lo:hi], ADD)
+        for lo, hi in pieces:
+            nc.vector.tensor_tensor(res[1][:, lo:hi], back[1][:, lo:hi], pair[:, lo:hi], ADD)
+            nc.sync.dma_start(out[P : 2 * P, lo:hi], res[1][:, lo:hi])

@@ -57,11 +57,10 @@ def tile_moe_tk_lin_none_kernel(
         offs_list = keep.tile([P, SLOTS // 16], U16, name="offs_list")
         pos_lists = [keep.tile([P, T // 16], U16, name="pos%d_list" % r) for r in range(TOP)]
 
-        first = [tile([P, 4, P], F32, "first%d" % c) for c in range(3)]
         first_bf = [tile([P, P, 4], BF16, "first_bf%d" % c) for c in range(2)]
         s4_bytes = E * PASSES4 * N
         first_bf.append(held.tile([P, P, 4], BF16, name="first_bf2", align_bytes=64, offset=s4_bytes - 512))
-        raw = {a: tile([P, 4, T], F32, "raw%d" % a) for a in ORDER[1:-1]}
+        raw = {a: tile([P, 4, T], F32, "raw%d" % a) for a in ORDER[:-1]}
         raw[4] = spread.tile([P, 4, T], F32, name="raw4", align_bytes=64, offset=0)
         gate_rows = tile([P, T], F32, "gate_rows")
 
@@ -86,8 +85,7 @@ def tile_moe_tk_lin_none_kernel(
 
         def load_x(a, lo, hi):
             rows = xT[512 * a : 512 * (a + 1), :].rearrange("(p j) w -> p j w", j=4)
-            dst = first[lo // P][:] if a == ORDER[0] else raw[a][:, :, lo:hi]
-            nc.sync.dma_start(dst, rows[:, :, lo:hi])
+            nc.sync.dma_start(raw[a][:, :, lo:hi], rows[:, :, lo:hi])
 
         def load_s4(r):
             src = w4_scales.rearrange("e a (q r) n -> r q (e a) n", r=4)[r]
@@ -104,6 +102,10 @@ def tile_moe_tk_lin_none_kernel(
         def load_w8(a, h, lo, hi):
             src = w8_words[lo:hi, a, :, P * h : P * (h + 1), :].rearrange("e p n r -> p e (n r)")
             nc.sync.dma_start(w[a, h][:, lo:hi, :].bitcast(I32), src.bitcast(I32))
+
+        def load_w0(lo, hi):
+            src = w8_words[lo:hi, 0].rearrange("e p n r -> p e (n r)")
+            nc.sync.dma_start(w[0][:, lo:hi, :].bitcast(I32), src.bitcast(I32))
 
         def turn(dst, src, on_vector=False):
             src = src.rearrange("p j (c i) -> p c j i", i=4)
@@ -139,8 +141,7 @@ def tile_moe_tk_lin_none_kernel(
             for r in range(4):
                 nc.sync.dma_start(moved[a][r:P:32, :].bitcast(I32), bytes_g[MOVED[a] + r : P : 32, :].bitcast(I32))
 
-        for c in range(3):
-            load_x(3, P * c, P * (c + 1))
+        load_x(3, 0, T)
         nc.sync.dma_start(offs_list[:], offs)
         for a in ORDER[1:]:
             load_x(a, 0, T)
@@ -201,16 +202,14 @@ def tile_moe_tk_lin_none_kernel(
             else:
                 nc.scalar.activation(dst, src, COPY)
 
-        turn(first_bf[0], first[0][:])
-        s8 = tile([P, E, N], U8, "s8", tag="first0")
+        for c in range(3):
+            turn(first_bf[c], raw[3][:, :, P * c : P * (c + 1)], on_vector=c < 2)
+        for c in range(3):
+            quantise_part(3, first_bf[c], P * c, P * (c + 1))
+        s8 = tile([P, E, N], U8, "s8", tag="raw3")
         for a in range(PASSES8):
             for r in range(4):
                 load_s8(a, r)
-        turn(first_bf[1], first[1][:], on_vector=True)
-        quantise_part(3, first_bf[0], 0, P)
-        turn(first_bf[2], first[2][:], on_vector=True)
-        quantise_part(3, first_bf[1], P, 2 * P)
-        quantise_part(3, first_bf[2], 2 * P, T)
         nc.sync.dma_start(packed[FIFTH:P, 0:T].bitcast(I32), planes[0 : P - FIFTH, T : 2 * T].bitcast(I32))
         s4 = held.tile([P, E * PASSES4, N], U8, name="s4", align_bytes=64, offset=0)
         for r in range(4):
@@ -242,7 +241,7 @@ def tile_moe_tk_lin_none_kernel(
         for q in range(0, P, 32):
             nc.vector.tensor_copy(out=packed[q : q + FIFTH, 0:T].bitcast(I32), in_=planes[q : q + FIFTH, 0:T].bitcast(I32))
         nc.vector.tensor_copy(out=bytes_g[:], in_=packed[:].indirect(offs_list[:]))
-        scale_bytes = {(0, 0): bytes_g, (0, 1): bytes_g, (0, 2): bytes_g, (1, 2): bytes_g}
+        scale_bytes = {(0, 0): bytes_g, (0, 1): bytes_g, (1, 0): bytes_g, (0, 2): bytes_g, (1, 2): bytes_g}
         move(3)
         w[4] = overlay.tile([P, E, 2 * N], U8, name="w4", align_bytes=64, offset=0)
         load_w(4, 0, E)
@@ -254,14 +253,15 @@ def tile_moe_tk_lin_none_kernel(
             for b, place in enumerate(places):
                 banks[h, b] = bank(place, [P, 512], "sums%d_%d" % (h, b))
         products(2)
-        w[0, 0] = tile([P, E, 2 * N], U8, "w00", tag="big0")
-        load_w8(0, 0, 0, E)
+        w[0] = tile([P, E, 4 * N], U8, "w0", tag="big0")
+        for h in range(HALVES):
+            w[0, h] = w[0][:, :, 4 * P * h : 4 * P * (h + 1)]
+        for lo in range(0, E, 6):
+            load_w0(lo, lo + 6)
         w[1, 0] = held.tile([P, E, 2 * N], U8, name="w10", align_bytes=64, offset=s4_bytes)
         for lo in range(0, E, 4):
             load_w8(1, 0, lo, lo + 4)
         products(3)
-        w[0, 1] = tile([P, E, 2 * N], U8, "w01", tag="words3")
-        load_w8(0, 1, 0, E)
         w[1, 1] = tile([P, E, 2 * N], U8, "w11", tag="raw2")
         for lo in range(0, E, 4):
             load_w8(1, 1, lo, lo + 4)
@@ -269,24 +269,21 @@ def tile_moe_tk_lin_none_kernel(
         products(4)
         gather_words(0, 0, EARLY)
         gather_words(0, EARLY, SLOTS)
-        for e in range(E):
-            product(e, 0, 0)
+        products(0)
         for experts in BANKS[0]:
             gather_words(1, C * experts[0], C * (experts[-1] + 1))
             for e in experts:
                 product(e, 0, 1)
         again = tile([P, SLOTS], U8, "again", tag="codes")
         nc.vector.tensor_copy(out=again[:].bitcast(I32), in_=bytes_g[:].bitcast(I32))
-        scale_bytes[1, 0] = again
         scale_bytes[1, 1] = again
         last = len(BANKS[0]) - 1
         for b in range(last):
             empty(0, b)
         empty(0, last, on_vector=True)
         for b, experts in enumerate(BANKS[1]):
-            for a in range(PASSES8):
-                for e in experts:
-                    product(e, 1, a)
+            for e in experts:
+                product(e, 1, 1)
             empty(1, b)
 
         def fetch(h, r, lo=0, hi=T):

@@ -38,6 +38,7 @@ BANKS = (
     ((0, 1, 2, 3), (4, 5, 6, 7), (8, 9, 10, 11)),
 )
 EARLY = 1024
+AHEAD = 4
 
 
 def tile_moe_tk_lin_none_kernel(
@@ -68,8 +69,8 @@ def tile_moe_tk_lin_none_kernel(
         small = {a: tile([P, 128, 4], BF16, "small%d" % a) for a in ORDER[1:]}
         codes = tile([P, (PASSES - 1) * T + WIDE], U32, "codes")
         planes = tile([P, PLANES * T], U8, "planes")
-        weight_bytes = 2 * N * E
-        packed = overlay.tile([P, WIDE], U8, name="packed", align_bytes=64, offset=0)
+        weight_bytes = 2 * N * (E - AHEAD)
+        packed = overlay.tile([P, WIDE], U8, name="packed", align_bytes=64, offset=weight_bytes - WIDE // 2)
         words = {3: tile([P, SLOTS], U32, "words3")}
         bytes_g = tile([P, SLOTS], U8, "bytes_g")
         moved = {a: tile([P, SLOTS], U8, "moved%d" % a) for a in MOVED}
@@ -95,9 +96,9 @@ def tile_moe_tk_lin_none_kernel(
             src = w8_scales[:, a].rearrange("e (q r) n -> r q e n", r=4)[r]
             nc.gpsimd.dma_start(s8[PLACE[a][1] + r : P : 32, :, :].bitcast(I32), src.bitcast(I32))
 
-        def load_w(a, lo, hi):
+        def load_w(dst, a, lo, hi):
             src = w4_words[lo:hi, a - PASSES8].rearrange("e p b -> p e b")
-            nc.sync.dma_start(w[a][:, lo:hi, :].bitcast(I32), src.bitcast(I32))
+            nc.sync.dma_start(dst[:].bitcast(I32), src.bitcast(I32))
 
         def load_w8(a, h, lo, hi):
             src = w8_words[lo:hi, a, :, P * h : P * (h + 1), :].rearrange("e p n r -> p e (n r)")
@@ -143,10 +144,11 @@ def tile_moe_tk_lin_none_kernel(
 
         load_x(3, 0, T)
         nc.sync.dma_start(offs_list[:], offs)
-        for a in ORDER[1:]:
-            load_x(a, 0, T)
+        load_x(ORDER[1], 0, T)
         for r, pos in enumerate((pos1, pos2, pos3, pos4)):
             nc.sync.dma_start(pos_lists[r][:], pos)
+        for a in ORDER[2:]:
+            load_x(a, 0, T)
         nc.vector.memset(gate_rows[:], 0.0)
         nc.sync.dma_start(gate_rows[0:TOP, :], gate[:, 0, :])
         make_identity(nc, ident[:])
@@ -175,7 +177,8 @@ def tile_moe_tk_lin_none_kernel(
                 lhsT = w[a, h][:, e, :].bitcast(FP8X4)
                 lhsT_scale = s8[row:P, e, ch]
             else:
-                lhsT = w[a][:, e, 2 * P * h : 2 * P * (h + 1)].bitcast(FP4X4)
+                row_of_e = w[a][:, e, :] if a != 4 else ahead[:, e, :] if e < AHEAD else w[a][:, e - AHEAD, :]
+                lhsT = row_of_e[:, 2 * P * h : 2 * P * (h + 1)].bitcast(FP4X4)
                 lhsT_scale = s4[:, PASSES4 * e + a - PASSES8, ch]
             nc.tensor.matmul_mx(
                 out=banks[h, b][:, C * col : C * (col + 1)],
@@ -215,7 +218,7 @@ def tile_moe_tk_lin_none_kernel(
         for r in range(4):
             load_s4(r)
         w[2] = held.tile([P, E, 2 * N], U8, name="w2", align_bytes=64, offset=s4_bytes)
-        load_w(2, 0, E)
+        load_w(w[2], 2, 0, E)
         for a in ORDER[1:]:
             turn(big[a], raw[a][:, :, 0:256])
             turn(small[a], raw[a][:, :, 256:T])
@@ -230,7 +233,9 @@ def tile_moe_tk_lin_none_kernel(
             nc.scalar.activation(g[:], wide[r][:], COPY)
             gates.append(g)
         w[3] = tile([P, E, 2 * N], U8, "w3", tag="raw2")
-        load_w(3, 0, E)
+        load_w(w[3], 3, 0, E)
+        ahead = tile([P, AHEAD, 2 * N], U8, "ahead", tag="raw0")
+        load_w(ahead, 4, 0, AHEAD)
         gather_words(3, 0, SLOTS)
         words[2] = tile([P, SLOTS], U32, "words2", tag="big0")
         quantise(2)
@@ -243,9 +248,14 @@ def tile_moe_tk_lin_none_kernel(
         nc.vector.tensor_copy(out=bytes_g[:], in_=packed[:].indirect(offs_list[:]))
         scale_bytes = {(0, 0): bytes_g, (0, 1): bytes_g, (1, 0): bytes_g, (0, 2): bytes_g, (1, 2): bytes_g}
         move(3)
-        w[4] = overlay.tile([P, E, 2 * N], U8, name="w4", align_bytes=64, offset=0)
-        load_w(4, 0, E)
+        w[4] = overlay.tile([P, E - AHEAD, 2 * N], U8, name="w4", align_bytes=64, offset=0)
+        load_w(w[4], 4, AHEAD, E)
         move(4)
+        w[0] = overlay.tile([P, E, 4 * N], U8, name="w0", align_bytes=64, offset=weight_bytes)
+        for h in range(HALVES):
+            w[0, h] = w[0][:, :, 4 * P * h : 4 * P * (h + 1)]
+        for lo in range(0, E, 6):
+            load_w0(lo, lo + 6)
         late_words = tile([P, len(LATE), SLOTS], U32, "late_words", tag="planes")
         for i, a in enumerate(LATE):
             words[a] = late_words[:, i, :]
@@ -253,14 +263,9 @@ def tile_moe_tk_lin_none_kernel(
             for b, place in enumerate(places):
                 banks[h, b] = bank(place, [P, 512], "sums%d_%d" % (h, b))
         products(2)
-        w[0] = tile([P, E, 4 * N], U8, "w0", tag="big0")
-        for h in range(HALVES):
-            w[0, h] = w[0][:, :, 4 * P * h : 4 * P * (h + 1)]
-        for lo in range(0, E, 6):
-            load_w0(lo, lo + 6)
         w[1, 0] = held.tile([P, E, 2 * N], U8, name="w10", align_bytes=64, offset=s4_bytes)
-        for lo in range(0, E, 4):
-            load_w8(1, 0, lo, lo + 4)
+        for lo, hi in ((0, 4), (4, 8), (8, 10), (10, E)):
+            load_w8(1, 0, lo, hi)
         products(3)
         w[1, 1] = tile([P, E, 2 * N], U8, "w11", tag="raw2")
         for lo in range(0, E, 4):

@@ -23,21 +23,22 @@ PASSES = 5
 PASSES8 = 2
 PASSES4 = 3
 HALVES = N // P
+BLOCKS = T // P
 FLOPS = 2 * SLOTS * K * N
 
 ORDER = (3, 2, 0, 1, 4)
-SUM_ORDER = (2, 3, 4, 0, 1)
-LATE = ORDER[2:]
+SUM_ORDER = (2, 0, 3, 4, 1)
+LATE = (0, 4, 1)
 WIDE = 2048
-PLACE = {2: (0, 0), 0: (0, 4), 1: (0, 8), 4: (0, 12), 3: (1, 0)}
-PLANES = 2
-FIFTH = 16
-MOVED = {3: FIFTH, 4: 12}
+ROW = {2: 0, 0: 4, 1: 8, 4: 12, 3: 0}
+MOVED = (4, 3)
+SHIFT = ROW[4] + 16
 BANKS = (
     ((0, 1, 2, 3), (4, 5, 6, 7), (8, 9), (10,), (11,)),
     ((0, 1, 2, 3), (4, 5, 6, 7), (8, 9, 10, 11)),
 )
 EARLY = 1024
+WHOLE = 4
 AHEAD = 4
 
 
@@ -47,66 +48,58 @@ def tile_moe_tk_lin_none_kernel(
     nc = tc.nc
     with ExitStack() as ctx:
         keep = ctx.enter_context(tc.tile_pool(name="keep", bufs=1))
-        overlay = ctx.enter_context(tc.tile_pool(name="overlay", bufs=1))
         held = ctx.enter_context(tc.tile_pool(name="held", bufs=1))
+        overlay = ctx.enter_context(tc.tile_pool(name="overlay", bufs=1))
         spread = ctx.enter_context(tc.tile_pool(name="spread", bufs=1))
         psum = ctx.enter_context(tc.psum_pool(name="psum", bufs=1))
 
         def tile(shape, dtype, name, tag=""):
             return keep.tile(shape, dtype, name=name, tag=tag or name, align_bytes=64)
 
+        def bank(index, shape, name):
+            return psum.tile(shape, F32, name=name, tag="bank%d" % index)
+
         offs_list = keep.tile([P, SLOTS // 16], U16, name="offs_list")
         pos_lists = [keep.tile([P, T // 16], U16, name="pos%d_list" % r) for r in range(TOP)]
 
-        first_bf = [tile([P, P, 4], BF16, "first_bf%d" % c) for c in range(2)]
         s4_bytes = E * PASSES4 * N
+        late4_bytes = 2 * N * (2 * E - AHEAD)
+        first_bf = [tile([P, P, 4], BF16, "first_bf%d" % c) for c in range(2)]
         first_bf.append(held.tile([P, P, 4], BF16, name="first_bf2", align_bytes=64, offset=s4_bytes - 512))
         raw = {a: tile([P, 4, T], F32, "raw%d" % a) for a in ORDER[:-1]}
         raw[4] = spread.tile([P, 4, T], F32, name="raw4", align_bytes=64, offset=0)
         gate_rows = tile([P, T], F32, "gate_rows")
-
         big = {a: tile([P, 256, 4], BF16, "big%d" % a) for a in ORDER[1:]}
         small = {a: tile([P, 128, 4], BF16, "small%d" % a) for a in ORDER[1:]}
         codes = tile([P, (PASSES - 1) * T + WIDE], U32, "codes")
-        planes = tile([P, PLANES * T], U8, "planes")
-        weight_bytes = 2 * N * (E - AHEAD)
-        packed = overlay.tile([P, WIDE], U8, name="packed", align_bytes=64, offset=weight_bytes - WIDE // 2)
+        planes = tile([P, 2 * T], U8, "planes")
+        packed = overlay.tile([P, WIDE], U8, name="packed", align_bytes=64, offset=late4_bytes - WIDE // 2)
         words = {3: tile([P, SLOTS], U32, "words3")}
         bytes_g = tile([P, SLOTS], U8, "bytes_g")
-        moved = {a: tile([P, SLOTS], U8, "moved%d" % a) for a in MOVED}
-        w = {}
+        moved = tile([P, len(MOVED), SLOTS], U8, "moved")
+        s8 = tile([P, PASSES8, E, N], U8, "s8")
         y = [tile([P, SLOTS], F32, "y%d" % h) for h in range(HALVES)]
         prod = [[tile([P, T], F32, "prod%d_%d" % (h, r)) for r in range(TOP)] for h in range(HALVES)]
-        turned = [tile([P, T], F32, "turned%d" % h) for h in range(HALVES)]
+        turned = tile([P, T], F32, "turned")
         ident = tile([P, P], F32, "ident")
         res = [tile([P, T], F32, "res%d" % h) for h in range(HALVES)]
+        pair = tile([P, T], F32, "pair")
+        three = tile([P, T], F32, "three")
+        w = {}
 
         def home(a):
             return T * (PASSES - 1 - ORDER.index(a))
 
-        def load_x(a, lo, hi):
-            rows = xT[512 * a : 512 * (a + 1), :].rearrange("(p j) w -> p j w", j=4)
-            nc.sync.dma_start(raw[a][:, :, lo:hi], rows[:, :, lo:hi])
+        def load_x(a):
+            nc.sync.dma_start(raw[a][:], xT[512 * a : 512 * (a + 1), :].rearrange("(p j) w -> p j w", j=4))
 
-        def load_s4(r):
-            src = w4_scales.rearrange("e a (q r) n -> r q (e a) n", r=4)[r]
-            nc.sync.dma_start(s4[r:P:32, :, :].bitcast(I32), src.bitcast(I32))
-
-        def load_s8(a, r):
-            src = w8_scales[:, a].rearrange("e (q r) n -> r q e n", r=4)[r]
-            nc.gpsimd.dma_start(s8[PLACE[a][1] + r : P : 32, :, :].bitcast(I32), src.bitcast(I32))
-
-        def load_w(dst, a, lo, hi):
+        def load_w4(dst, a, lo, hi):
             src = w4_words[lo:hi, a - PASSES8].rearrange("e p b -> p e b")
-            nc.sync.dma_start(dst[:].bitcast(I32), src.bitcast(I32))
+            nc.sync.dma_start(dst.bitcast(I32), src.bitcast(I32))
 
-        def load_w8(a, h, lo, hi):
-            src = w8_words[lo:hi, a, :, P * h : P * (h + 1), :].rearrange("e p n r -> p e (n r)")
-            nc.sync.dma_start(w[a, h][:, lo:hi, :].bitcast(I32), src.bitcast(I32))
-
-        def load_w0(lo, hi):
-            src = w8_words[lo:hi, 0].rearrange("e p n r -> p e (n r)")
-            nc.sync.dma_start(w[0][:, lo:hi, :].bitcast(I32), src.bitcast(I32))
+        def load_w8(dst, a, lo, hi, n0=0, n1=N):
+            src = w8_words[lo:hi, a, :, n0:n1, :].rearrange("e p n r -> p e (n r)")
+            nc.sync.dma_start(dst[:, :, 4 * n0 : 4 * n1].bitcast(I32), src.bitcast(I32))
 
         def turn(dst, src, on_vector=False):
             src = src.rearrange("p j (c i) -> p c j i", i=4)
@@ -117,10 +110,10 @@ def tile_moe_tk_lin_none_kernel(
                 nc.scalar.activation(dst, src, COPY)
 
         def quantise_part(a, src, lo, hi):
-            i, row = PLACE[a]
+            at = T if a == ORDER[0] else 0
             nc.vector.quantize_mx(
                 out=codes[:, home(a) + lo : home(a) + hi].bitcast(FP8X4),
-                scales=planes[row:P, T * i + lo : T * i + hi],
+                scales=planes[ROW[a] : P, at + lo : at + hi],
                 in_=src[:].rearrange("p w j -> p (w j)"),
             )
 
@@ -128,64 +121,116 @@ def tile_moe_tk_lin_none_kernel(
             quantise_part(a, big[a], 0, 256)
             quantise_part(a, small[a], 256, T)
 
-        def width(count):
-            return 512 if count <= 384 else 1024 if count <= 768 else WIDE
-
-        def slots_of(a, lo, hi):
-            return words[a][:, lo:hi]
-
         def gather_words(a, lo, hi):
-            window = codes[:, home(a) : home(a) + width(hi - lo)]
-            nc.vector.tensor_copy(out=slots_of(a, lo, hi), in_=window.indirect(offs_list[:, lo // 16 : hi // 16]))
+            count = hi - lo
+            width = 512 if count <= 384 else 1024 if count <= 768 else WIDE
+            window = codes[:, home(a) : home(a) + width]
+            nc.vector.tensor_copy(out=words[a][:, lo:hi], in_=window.indirect(offs_list[:, lo // 16 : hi // 16]))
 
-        def move(a):
-            for r in range(4):
-                nc.sync.dma_start(moved[a][r:P:32, :].bitcast(I32), bytes_g[MOVED[a] + r : P : 32, :].bitcast(I32))
-
-        load_x(3, 0, T)
+        load_x(ORDER[0])
         nc.sync.dma_start(offs_list[:], offs)
-        load_x(ORDER[1], 0, T)
+        load_x(ORDER[1])
         for r, pos in enumerate((pos1, pos2, pos3, pos4)):
             nc.sync.dma_start(pos_lists[r][:], pos)
         for a in ORDER[2:]:
-            load_x(a, 0, T)
+            load_x(a)
         nc.vector.memset(gate_rows[:], 0.0)
         nc.sync.dma_start(gate_rows[0:TOP, :], gate[:, 0, :])
         make_identity(nc, ident[:])
+        for a in range(PASSES8):
+            for r in range(4):
+                src = w8_scales[:, a].rearrange("e (q r) n -> r q e n", r=4)[r]
+                nc.gpsimd.dma_start(s8[ROW[a] + r : P : 32, a, :, :].bitcast(I32), src.bitcast(I32))
         nc.vector.memset(planes[:].bitcast(I32), 0)
         nc.vector.memset(packed[:].bitcast(I32), 0)
         nc.vector.memset(codes[:, PASSES * T :].bitcast(I32), 0)
 
-        def bank(index, shape, name):
-            return psum.tile(shape, F32, name=name, tag="bank%d" % index)
-
-        by_token = bank(0, [P, T // P, P], "by_token")
-        for b in range(T // P):
+        by_token = bank(2, [P, BLOCKS, P], "by_token")
+        for b in range(BLOCKS):
             nc.tensor.transpose(by_token[:, b, :], gate_rows[:, P * b : P * (b + 1)], ident[:])
-        wide = [bank(1 + r, [P, T], "wide%d" % r) for r in range(TOP)]
+
+        for c in range(3):
+            turn(first_bf[c], raw[3][:, :, P * c : P * (c + 1)], on_vector=c < 2)
+        for c in range(3):
+            quantise_part(3, first_bf[c], P * c, P * (c + 1))
+        nc.sync.dma_start(packed[SHIFT:P, 0:T].bitcast(I32), planes[0 : P - SHIFT, T : 2 * T].bitcast(I32))
+        s4 = held.tile([P, E * PASSES4, N], U8, name="s4", align_bytes=64, offset=0)
+        for r in range(4):
+            src = w4_scales.rearrange("e a (q r) n -> r q (e a) n", r=4)[r]
+            nc.sync.dma_start(s4[r:P:32, :, :].bitcast(I32), src.bitcast(I32))
+        w[2] = held.tile([P, E, 2 * N], U8, name="w2", align_bytes=64, offset=s4_bytes)
+        load_w4(w[2][:], 2, 0, E)
+        for a in ORDER[1:]:
+            turn(big[a], raw[a][:, :, 0:256])
+            turn(small[a], raw[a][:, :, 256:T])
+
+        gate_cols = spread.tile([P, BLOCKS, TOP], F32, name="gate_cols", align_bytes=64, offset=0)
+        nc.scalar.activation(gate_cols[:], by_token[:, :, 0:TOP], COPY)
+        gates = []
+        for r in range(TOP - 1):
+            wide = bank((7, 0, 1)[r], [P, T], "wide%d" % r)
+            for b in range(BLOCKS):
+                column = gate_cols[:, b, r : r + 1].to_broadcast([P, P])
+                nc.tensor.transpose(wide[:, P * b : P * (b + 1)], column, ident[:])
+            g = spread.tile([P, T], F32, name="gate%d" % r, align_bytes=64, offset=64 + 4 * T * r)
+            nc.scalar.activation(g[:], wide[:], COPY)
+            gates.append(g)
+
+        w0_parts = [tile([P, E // 2, 4 * N], U8, "w0_%d" % i, tag="raw%d" % a) for i, a in enumerate((2, 0))]
+        for i, part in enumerate(w0_parts):
+            load_w8(part[:], 0, E // 2 * i, E // 2 * (i + 1))
+        ahead = tile([P, AHEAD, 2 * N], U8, "ahead", tag="raw1")
+        load_w4(ahead[:], 3, 0, AHEAD)
+
+        gather_words(3, 0, SLOTS)
+        words[2] = tile([P, SLOTS], U32, "words2", tag="big0")
+        quantise(2)
+        quantise(0)
+        gather_words(2, 0, SLOTS)
+        quantise(1)
+        quantise(4)
+        for q in range(0, P, 32):
+            nc.vector.tensor_copy(out=packed[q : q + 16, 0:T].bitcast(I32), in_=planes[q : q + 16, 0:T].bitcast(I32))
+        nc.vector.tensor_copy(out=bytes_g[:], in_=packed[:].indirect(offs_list[:]))
+        for r in range(4):
+            nc.sync.dma_start(moved[r:P:32, :, :].bitcast(I32), bytes_g[ROW[4] + r : P : 16, :].bitcast(I32))
+        late4 = overlay.tile([P, 2 * E - AHEAD, 2 * N], U8, name="late4", align_bytes=64, offset=0)
+        load_w4(late4[:, 0 : E - AHEAD, :], 3, AHEAD, E)
+        load_w4(late4[:, E - AHEAD :, :], 4, 0, E)
+        late_words = tile([P, len(LATE), SLOTS], U32, "late_words", tag="planes")
+        for i, a in enumerate(LATE):
+            words[a] = late_words[:, i, :]
 
         banks = {}
+        for h, places in enumerate(((5, 6, 7, 0, 1), (2, 3, 4))):
+            for b, place in enumerate(places):
+                banks[h, b] = bank(place, [P, 512], "sums%d_%d" % (h, b))
         home_bank = {(h, e): b for h in range(HALVES) for b, experts in enumerate(BANKS[h]) for e in experts}
 
         def product(e, h, a):
             ch = slice(P * h, P * (h + 1))
-            i, row = PLACE[a]
             b = home_bank[h, e]
             col = e - BANKS[h][b][0]
             s = slice(C * e, C * (e + 1))
             if a < PASSES8:
-                lhsT = w[a, h][:, e, :].bitcast(FP8X4)
-                lhsT_scale = s8[row:P, e, ch]
+                row_of_e = w[1][:, e, :] if a == 1 else w0_parts[e // (E // 2)][:, e % (E // 2), :]
+                lhsT = row_of_e[:, 4 * P * h : 4 * P * (h + 1)].bitcast(FP8X4)
+                lhsT_scale = s8[ROW[a] : P, a, e, ch]
             else:
-                row_of_e = w[a][:, e, :] if a != 4 else ahead[:, e, :] if e < AHEAD else w[a][:, e - AHEAD, :]
+                if a == 2:
+                    row_of_e = w[2][:, e, :]
+                elif a == 3 and e < AHEAD:
+                    row_of_e = ahead[:, e, :]
+                else:
+                    row_of_e = late4[:, E * (a - 3) + e - AHEAD, :]
                 lhsT = row_of_e[:, 2 * P * h : 2 * P * (h + 1)].bitcast(FP4X4)
                 lhsT_scale = s4[:, PASSES4 * e + a - PASSES8, ch]
             nc.tensor.matmul_mx(
                 out=banks[h, b][:, C * col : C * (col + 1)],
                 lhsT=lhsT,
                 lhsT_scale=lhsT_scale,
-                rhs=slots_of(a, C * e, C * (e + 1)).bitcast(FP8X4),
-                rhs_scale=moved[a][:, s] if a in MOVED else scale_bytes[h, a][row:P, s],
+                rhs=words[a][:, s].bitcast(FP8X4),
+                rhs_scale=moved[:, MOVED.index(a), s] if a in MOVED else bytes_g[ROW[a] : P, s],
                 start=(a == SUM_ORDER[0] and col == 0),
                 stop=(a == SUM_ORDER[-1] and e == BANKS[h][b][-1]),
             )
@@ -205,129 +250,83 @@ def tile_moe_tk_lin_none_kernel(
             else:
                 nc.scalar.activation(dst, src, COPY)
 
-        for c in range(3):
-            turn(first_bf[c], raw[3][:, :, P * c : P * (c + 1)], on_vector=c < 2)
-        for c in range(3):
-            quantise_part(3, first_bf[c], P * c, P * (c + 1))
-        s8 = tile([P, E, N], U8, "s8", tag="raw3")
-        for a in range(PASSES8):
-            for r in range(4):
-                load_s8(a, r)
-        nc.sync.dma_start(packed[FIFTH:P, 0:T].bitcast(I32), planes[0 : P - FIFTH, T : 2 * T].bitcast(I32))
-        s4 = held.tile([P, E * PASSES4, N], U8, name="s4", align_bytes=64, offset=0)
-        for r in range(4):
-            load_s4(r)
-        w[2] = held.tile([P, E, 2 * N], U8, name="w2", align_bytes=64, offset=s4_bytes)
-        load_w(w[2], 2, 0, E)
-        for a in ORDER[1:]:
-            turn(big[a], raw[a][:, :, 0:256])
-            turn(small[a], raw[a][:, :, 256:T])
-        gate_cols = spread.tile([P, T // P, TOP], F32, name="gate_cols", align_bytes=64, offset=0)
-        nc.scalar.activation(gate_cols[:], by_token[:, :, 0:TOP], COPY)
-        gates = []
-        for r in range(TOP):
-            for b in range(T // P):
-                column = gate_cols[:, b, r : r + 1].to_broadcast([P, P])
-                nc.tensor.transpose(wide[r][:, P * b : P * (b + 1)], column, ident[:])
-            g = spread.tile([P, T], F32, name="gate%d" % r, align_bytes=64, offset=64 + 4 * T * r)
-            nc.scalar.activation(g[:], wide[r][:], COPY)
-            gates.append(g)
-        w[3] = tile([P, E, 2 * N], U8, "w3", tag="raw2")
-        load_w(w[3], 3, 0, E)
-        ahead = tile([P, AHEAD, 2 * N], U8, "ahead", tag="raw0")
-        load_w(ahead, 4, 0, AHEAD)
-        gather_words(3, 0, SLOTS)
-        words[2] = tile([P, SLOTS], U32, "words2", tag="big0")
-        quantise(2)
-        quantise(0)
-        gather_words(2, 0, SLOTS)
-        quantise(1)
-        quantise(4)
-        for q in range(0, P, 32):
-            nc.vector.tensor_copy(out=packed[q : q + FIFTH, 0:T].bitcast(I32), in_=planes[q : q + FIFTH, 0:T].bitcast(I32))
-        nc.vector.tensor_copy(out=bytes_g[:], in_=packed[:].indirect(offs_list[:]))
-        scale_bytes = {(0, 0): bytes_g, (0, 1): bytes_g, (1, 0): bytes_g, (0, 2): bytes_g, (1, 2): bytes_g}
-        move(3)
-        w[4] = overlay.tile([P, E - AHEAD, 2 * N], U8, name="w4", align_bytes=64, offset=0)
-        load_w(w[4], 4, AHEAD, E)
-        move(4)
-        w[0] = overlay.tile([P, E, 4 * N], U8, name="w0", align_bytes=64, offset=weight_bytes)
-        for h in range(HALVES):
-            w[0, h] = w[0][:, :, 4 * P * h : 4 * P * (h + 1)]
-        for lo in range(0, E, 6):
-            load_w0(lo, lo + 6)
-        late_words = tile([P, len(LATE), SLOTS], U32, "late_words", tag="planes")
-        for i, a in enumerate(LATE):
-            words[a] = late_words[:, i, :]
-        for h, places in enumerate(((5, 6, 7, 0, 1), (2, 3, 4))):
-            for b, place in enumerate(places):
-                banks[h, b] = bank(place, [P, 512], "sums%d_%d" % (h, b))
         products(2)
-        w[1, 0] = held.tile([P, E, 2 * N], U8, name="w10", align_bytes=64, offset=s4_bytes)
-        for lo, hi in ((0, 4), (4, 8), (8, 10), (10, E)):
-            load_w8(1, 0, lo, hi)
-        products(3)
-        w[1, 1] = tile([P, E, 2 * N], U8, "w11", tag="raw2")
-        for lo in range(0, E, 4):
-            load_w8(1, 1, lo, lo + 4)
-        gather_words(4, 0, SLOTS)
-        products(4)
-        gather_words(0, 0, EARLY)
-        gather_words(0, EARLY, SLOTS)
-        products(0)
-        for experts in BANKS[0]:
+        w[1] = overlay.tile([P, E, 4 * N], U8, name="w1", align_bytes=64, offset=late4_bytes)
+        load_w8(w[1][:, 0:WHOLE, :], 1, 0, WHOLE)
+        for h, cuts in enumerate(((WHOLE, 8, 10, E), (WHOLE, 8, E))):
+            for lo, hi in zip(cuts, cuts[1:]):
+                load_w8(w[1][:, lo:hi, :], 1, lo, hi, P * h, P * (h + 1))
+        for a in (0, 3, 4):
+            if a in LATE:
+                gather_words(a, 0, EARLY)
+                gather_words(a, EARLY, SLOTS)
+            products(a)
+        last = len(BANKS[0]) - 1
+        for b, experts in enumerate(BANKS[0]):
             gather_words(1, C * experts[0], C * (experts[-1] + 1))
             for e in experts:
                 product(e, 0, 1)
-        again = tile([P, SLOTS], U8, "again", tag="codes")
-        nc.vector.tensor_copy(out=again[:].bitcast(I32), in_=bytes_g[:].bitcast(I32))
-        scale_bytes[1, 1] = again
-        last = len(BANKS[0]) - 1
-        for b in range(last):
-            empty(0, b)
-        empty(0, last, on_vector=True)
-        for b, experts in enumerate(BANKS[1]):
-            for e in experts:
-                product(e, 1, 1)
-            empty(1, b)
+            empty(0, b, on_vector=b == last)
+            if b == 0:
+                for e in experts:
+                    product(e, 1, 1)
+                empty(1, 0)
+
+        def fetch_plain(h):
+            nc.scalar.activation(prod[h][TOP - 1][:], y[h][:].indirect(pos_lists[TOP - 1][:]), COPY)
 
         def fetch(h, r, lo=0, hi=T):
             window = y[h][:].indirect(pos_lists[r][:, lo // 16 : hi // 16])
             nc.vector.tensor_tensor(prod[h][r][:, lo:hi], window, gates[r][:, lo:hi], MULT)
 
-        blocks = [slice(P * b, P * (b + 1)) for b in range(T // P)]
+        blocks = [slice(P * b, P * (b + 1)) for b in range(BLOCKS)]
 
         def add_turned(dst, src, start, stop):
             nc.tensor.matmul(dst, src, ident[:], start=start, stop=stop, is_transpose=True)
 
-        there = bank(4, [P, T], "there0")
-        for r in range(TOP):
+        def gate_turned(h, place):
+            plain = bank(place, [P, BLOCKS, P], "plain%d" % h)
+            for b, cols in enumerate(blocks):
+                nc.tensor.transpose(plain[:, b, :], prod[h][TOP - 1][:, cols], ident[:])
+            for b in range(BLOCKS):
+                nc.scalar.activation(gated[h][:, b, :], plain[:, b, :], COPY, scale=gate_cols[:, b, TOP - 1 : TOP])
+
+        gated = [
+            overlay.tile([P, BLOCKS, P], F32, name="gated0", align_bytes=64, offset=late4_bytes),
+            tile([P, BLOCKS, P], F32, "gated1"),
+        ]
+        fetch_plain(0)
+        for b, experts in list(enumerate(BANKS[1]))[1:]:
+            for e in experts:
+                product(e, 1, 1)
+            empty(1, b)
+        fetch_plain(1)
+        gate_turned(0, 5)
+        there = bank(3, [P, T], "there")
+        for r in range(TOP - 1):
             fetch(0, r)
-            for cols in blocks:
-                first_one = r == 0 and cols == blocks[0]
-                last_one = r == TOP - 1 and cols == blocks[-1]
-                add_turned(there[:, cols], prod[0][r][:, cols], first_one, last_one)
-        nc.scalar.activation(turned[0][:], there[:], COPY)
-        back = [bank(5, [P, T], "back0"), bank(1, [P, T], "back1")]
-        for cols in blocks:
-            nc.tensor.transpose(back[0][:, cols], turned[0][:, cols], ident[:])
+            for b, cols in enumerate(blocks):
+                add_turned(there[:, cols], prod[0][r][:, cols], r == 0 and b == 0, r == TOP - 2 and b == BLOCKS - 1)
+        nc.scalar.activation(turned[:], there[:], COPY)
+        gate_turned(1, 6)
+        back = [bank(0, [P, T], "back0"), bank(7, [P, T], "back1")]
+        for b, cols in enumerate(blocks):
+            add_turned(back[0][:, cols], gated[0][:, b, :], b == 0, False)
+        for b, cols in enumerate(blocks):
+            add_turned(back[0][:, cols], turned[:, cols], False, b == BLOCKS - 1)
+        for b, cols in enumerate(blocks):
+            nc.tensor.transpose(back[1][:, cols], gated[1][:, b, :], ident[:])
         nc.scalar.activation(res[0][:], back[0][:], COPY)
-        nc.sync.dma_start(out[0:P, :], res[0][:])
-        parts = [bank(place, [P, P], "there1_%d" % place) for place in (6, 7, 0)]
-        for r in range(2):
-            fetch(1, r)
-            for part, cols in zip(parts, blocks):
-                add_turned(part[:], prod[1][r][:, cols], r == 0, r == 1)
-        for part, cols in zip(parts, blocks):
-            nc.scalar.activation(turned[1][:, cols], part[:], COPY)
-            nc.tensor.transpose(back[1][:, cols], turned[1][:, cols], ident[:])
-        fetch(1, 2)
+        nc.scalar.dma_start(out[0:P, :], res[0][:])
+
         pieces = ((0, 256), (256, T))
-        pair = tile([P, T], F32, "pair")
+        fetch(1, 0)
+        fetch(1, 1)
+        fetch(1, 2, *pieces[0])
+        nc.vector.tensor_tensor(pair[:], prod[1][0][:], prod[1][1][:], ADD)
+        fetch(1, 2, *pieces[1])
         for lo, hi in pieces:
-            fetch(1, 3, lo, hi)
+            nc.vector.tensor_tensor(three[:, lo:hi], pair[:, lo:hi], prod[1][2][:, lo:hi], ADD)
         for lo, hi in pieces:
-            nc.vector.tensor_tensor(pair[:, lo:hi], prod[1][2][:, lo:hi], prod[1][3][:, lo:hi], ADD)
-        for lo, hi in pieces:
-            nc.vector.tensor_tensor(res[1][:, lo:hi], back[1][:, lo:hi], pair[:, lo:hi], ADD)
+            nc.vector.tensor_tensor(res[1][:, lo:hi], back[1][:, lo:hi], three[:, lo:hi], ADD)
             nc.sync.dma_start(out[P : 2 * P, lo:hi], res[1][:, lo:hi])

@@ -77,7 +77,6 @@ def tile_moe_tk_lin_none_kernel(
         words = {3: tile([P, SLOTS], U32, "words3")}
         bytes_g = tile([P, SLOTS], U8, "bytes_g")
         moved = tile([P, len(MOVED), SLOTS], U8, "moved")
-        s8 = tile([P, PASSES8, E, N], U8, "s8")
         y = [tile([P, SLOTS], F32, "y%d" % h) for h in range(HALVES)]
         prod = [[tile([P, T], F32, "prod%d_%d" % (h, r)) for r in range(TOP)] for h in range(HALVES)]
         turned = tile([P, T], F32, "turned")
@@ -137,10 +136,6 @@ def tile_moe_tk_lin_none_kernel(
         nc.vector.memset(gate_rows[:], 0.0)
         nc.sync.dma_start(gate_rows[0:TOP, :], gate[:, 0, :])
         make_identity(nc, ident[:])
-        for a in range(PASSES8):
-            for r in range(4):
-                src = w8_scales[:, a].rearrange("e (q r) n -> r q e n", r=4)[r]
-                nc.gpsimd.dma_start(s8[ROW[a] + r : P : 32, a, :, :].bitcast(I32), src.bitcast(I32))
         nc.vector.memset(planes[:].bitcast(I32), 0)
         nc.vector.memset(packed[:].bitcast(I32), 0)
         nc.vector.memset(codes[:, PASSES * T :].bitcast(I32), 0)
@@ -153,6 +148,11 @@ def tile_moe_tk_lin_none_kernel(
             turn(first_bf[c], raw[3][:, :, P * c : P * (c + 1)], on_vector=c < 2)
         for c in range(3):
             quantise_part(3, first_bf[c], P * c, P * (c + 1))
+        s8 = tile([P, PASSES8, E, N], U8, "s8", tag="raw3")
+        for a in range(PASSES8):
+            for r in range(4):
+                src = w8_scales[:, a].rearrange("e (q r) n -> r q e n", r=4)[r]
+                nc.gpsimd.dma_start(s8[ROW[a] + r : P : 32, a, :, :].bitcast(I32), src.bitcast(I32))
         nc.sync.dma_start(packed[SHIFT:P, 0:T].bitcast(I32), planes[0 : P - SHIFT, T : 2 * T].bitcast(I32))
         s4 = held.tile([P, E * PASSES4, N], U8, name="s4", align_bytes=64, offset=0)
         for r in range(4):

@@ -195,8 +195,10 @@ def tile_moe_tk_lin_none_kernel(
         for r in range(4):
             nc.sync.dma_start(moved[r:P:32, :, :].bitcast(I32), bytes_g[ROW[4] + r : P : 16, :].bitcast(I32))
         late4 = overlay.tile([P, 2 * E - AHEAD, 2 * N], U8, name="late4", align_bytes=64, offset=0)
-        load_w4(late4[:, 0 : E - AHEAD, :], 3, AHEAD, E)
-        load_w4(late4[:, E - AHEAD :, :], 4, 0, E)
+        for a, first in ((3, AHEAD), (4, 0)):
+            for lo in range(first, E, 4):
+                at = E * (a - 3) + lo - AHEAD
+                load_w4(late4[:, at : at + 4, :], a, lo, lo + 4)
         late_words = tile([P, len(LATE), SLOTS], U32, "late_words", tag="planes")
         for i, a in enumerate(LATE):
             words[a] = late_words[:, i, :]

@@ -191,7 +191,9 @@ def tile_moe_tk_lin_none_kernel(
         quantise(4)
         for q in range(0, P, 32):
             nc.vector.tensor_copy(out=packed[q : q + 16, 0:T].bitcast(I32), in_=planes[q : q + 16, 0:T].bitcast(I32))
-        nc.vector.tensor_copy(out=bytes_g[:], in_=packed[:].indirect(offs_list[:]))
+        for lo in range(0, SLOTS, SLOTS // 2):
+            hi = lo + SLOTS // 2
+            nc.vector.tensor_copy(out=bytes_g[:, lo:hi], in_=packed[:].indirect(offs_list[:, lo // 16 : hi // 16]))
         for r in range(4):
             nc.sync.dma_start(moved[r:P:32, :, :].bitcast(I32), bytes_g[ROW[4] + r : P : 16, :].bitcast(I32))
         late4 = overlay.tile([P, 2 * E - AHEAD, 2 * N], U8, name="late4", align_bytes=64, offset=0)
@@ -252,7 +254,10 @@ def tile_moe_tk_lin_none_kernel(
             else:
                 nc.scalar.activation(dst, src, COPY)
 
-        products(2)
+        for lo in range(0, E, E // 2):
+            for h in range(HALVES):
+                for e in range(lo, lo + E // 2):
+                    product(e, h, 2)
         w[1] = overlay.tile([P, E, 4 * N], U8, name="w1", align_bytes=64, offset=late4_bytes)
         load_w8(w[1][:, 0:WHOLE, :], 1, 0, WHOLE)
         for h, cuts in enumerate(((WHOLE, 8, 10, E), (WHOLE, 8, E))):

@@ -32,7 +32,7 @@ LATE = (0, 4, 1)
 WIDE = 2048
 ROW = {2: 0, 0: 4, 1: 8, 4: 12, 3: 0}
 MOVED = (4, 3)
-SHIFT = ROW[4] + 16
+TOP_ROWS = P - 16
 BANKS = (
     ((0, 1, 2, 3), (4, 5, 6, 7), (8, 9), (10,), (11,)),
     ((0, 1, 2, 3), (4, 5, 6, 7), (8, 9, 10, 11)),
@@ -76,7 +76,7 @@ def tile_moe_tk_lin_none_kernel(
         packed = overlay.tile([P, WIDE], U8, name="packed", align_bytes=64, offset=late4_bytes - WIDE // 2)
         words = {3: tile([P, SLOTS], U32, "words3")}
         bytes_g = tile([P, SLOTS], U8, "bytes_g")
-        moved = tile([P, len(MOVED), SLOTS], U8, "moved")
+        moved = {a: tile([P, SLOTS], U8, "moved%d" % a) for a in MOVED}
         y = [tile([P, SLOTS], F32, "y%d" % h) for h in range(HALVES)]
         prod = [[tile([P, T], F32, "prod%d_%d" % (h, r)) for r in range(TOP)] for h in range(HALVES)]
         turned = tile([P, T], F32, "turned")
@@ -153,13 +153,14 @@ def tile_moe_tk_lin_none_kernel(
             for r in range(4):
                 src = w8_scales[:, a].rearrange("e (q r) n -> r q e n", r=4)[r]
                 nc.gpsimd.dma_start(s8[ROW[a] + r : P : 32, a, :, :].bitcast(I32), src.bitcast(I32))
-        nc.sync.dma_start(packed[SHIFT:P, 0:T].bitcast(I32), planes[0 : P - SHIFT, T : 2 * T].bitcast(I32))
+        for r in range(4):
+            nc.sync.dma_start(packed[TOP_ROWS + r : P : 4, 0:T].bitcast(I32), planes[r:P:32, T : 2 * T].bitcast(I32))
+        w[2] = held.tile([P, E, 2 * N], U8, name="w2", align_bytes=64, offset=s4_bytes)
+        load_w4(w[2][:], 2, 0, E)
         s4 = held.tile([P, E * PASSES4, N], U8, name="s4", align_bytes=64, offset=0)
         for r in range(4):
             src = w4_scales.rearrange("e a (q r) n -> r q (e a) n", r=4)[r]
             nc.sync.dma_start(s4[r:P:32, :, :].bitcast(I32), src.bitcast(I32))
-        w[2] = held.tile([P, E, 2 * N], U8, name="w2", align_bytes=64, offset=s4_bytes)
-        load_w4(w[2][:], 2, 0, E)
         for a in ORDER[1:]:
             turn(big[a], raw[a][:, :, 0:256])
             turn(small[a], raw[a][:, :, 256:T])
@@ -189,18 +190,20 @@ def tile_moe_tk_lin_none_kernel(
         gather_words(2, 0, SLOTS)
         quantise(1)
         quantise(4)
-        for q in range(0, P, 32):
-            nc.vector.tensor_copy(out=packed[q : q + 16, 0:T].bitcast(I32), in_=planes[q : q + 16, 0:T].bitcast(I32))
+        nc.vector.tensor_copy(out=packed[0:TOP_ROWS, 0:T].bitcast(I32), in_=planes[0:TOP_ROWS, 0:T].bitcast(I32))
         for lo in range(0, SLOTS, SLOTS // 2):
             hi = lo + SLOTS // 2
             nc.vector.tensor_copy(out=bytes_g[:, lo:hi], in_=packed[:].indirect(offs_list[:, lo // 16 : hi // 16]))
         for r in range(4):
-            nc.sync.dma_start(moved[r:P:32, :, :].bitcast(I32), bytes_g[ROW[4] + r : P : 16, :].bitcast(I32))
+            nc.sync.dma_start(moved[3][r:P:32, :].bitcast(I32), bytes_g[TOP_ROWS + r : P : 4, :].bitcast(I32))
         late4 = overlay.tile([P, 2 * E - AHEAD, 2 * N], U8, name="late4", align_bytes=64, offset=0)
-        for a, first in ((3, AHEAD), (4, 0)):
-            for lo in range(first, E, 4):
-                at = E * (a - 3) + lo - AHEAD
-                load_w4(late4[:, at : at + 4, :], a, lo, lo + 4)
+        groups = [(a, lo) for a, first in ((3, AHEAD), (4, 0)) for lo in range(first, E, 4)]
+        for i, (a, lo) in enumerate(groups):
+            if i == len(groups) - 1:
+                for r in range(4):
+                    nc.sync.dma_start(moved[4][r:P:32, :].bitcast(I32), bytes_g[ROW[4] + r : P : 32, :].bitcast(I32))
+            at = E * (a - 3) + lo - AHEAD
+            load_w4(late4[:, at : at + 4, :], a, lo, lo + 4)
         late_words = tile([P, len(LATE), SLOTS], U32, "late_words", tag="planes")
         for i, a in enumerate(LATE):
             words[a] = late_words[:, i, :]
@@ -234,7 +237,7 @@ def tile_moe_tk_lin_none_kernel(
                 lhsT=lhsT,
                 lhsT_scale=lhsT_scale,
                 rhs=words[a][:, s].bitcast(FP8X4),
-                rhs_scale=moved[:, MOVED.index(a), s] if a in MOVED else bytes_g[ROW[a] : P, s],
+                rhs_scale=moved[a][:, s] if a in MOVED else bytes_g[ROW[a] : P, s],
                 start=(a == SUM_ORDER[0] and col == 0),
                 stop=(a == SUM_ORDER[-1] and e == BANKS[h][b][-1]),
             )

from contextlib import ExitStack

import concourse.mybir as mybir
from concourse.masks import make_identity

F32 = mybir.dt.float32
BF16 = mybir.dt.bfloat16
I32 = mybir.dt.int32
U32 = mybir.dt.uint32
U16 = mybir.dt.uint16
U8 = mybir.dt.uint8
FP8X4 = mybir.dt.float8_e4m3fn_x4
FP4X4 = mybir.dt.float4_e2m1fn_x4
COPY = mybir.ActivationFunctionType.Copy
MULT = mybir.AluOpType.mult
ADD = mybir.AluOpType.add

P = 128
K, T, E, C, N = 2560, 384, 12, 128, 256
TOP = 4
SLOTS = E * C
PASSES = 5
PASSES8 = 2
PASSES4 = 3
HALVES = N // P
BLOCKS = T // P
FLOPS = 2 * SLOTS * K * N

ORDER = (3, 2, 0, 1, 4)
SUM_ORDER = (2, 0, 3, 4, 1)
LATE = (0, 4, 1)
WIDE = 2048
ROW = {2: 0, 0: 4, 1: 8, 4: 12, 3: 0}
MOVED = (4, 3)
TOP_ROWS = P - 16
BANKS = (
    ((0, 1, 2, 3), (4, 5, 6, 7), (8, 9), (10,), (11,)),
    ((0, 1, 2, 3), (4, 5, 6, 7), (8, 9, 10, 11)),
)
EARLY = 1024
WHOLE = 4
AHEAD = 4


def tile_moe_tk_lin_none_kernel(
    tc, xT, w8_words, w8_scales, w4_words, w4_scales, gate, offs, pos1, pos2, pos3, pos4, out
):
    nc = tc.nc
    with ExitStack() as ctx:
        keep = ctx.enter_context(tc.tile_pool(name="keep", bufs=1))
        held = ctx.enter_context(tc.tile_pool(name="held", bufs=1))
        overlay = ctx.enter_context(tc.tile_pool(name="overlay", bufs=1))
        spread = ctx.enter_context(tc.tile_pool(name="spread", bufs=1))
        psum = ctx.enter_context(tc.psum_pool(name="psum", bufs=1))

        def tile(shape, dtype, name, tag=""):
            return keep.tile(shape, dtype, name=name, tag=tag or name, align_bytes=64)

        def bank(index, shape, name):
            return psum.tile(shape, F32, name=name, tag="bank%d" % index)

        offs_list = keep.tile([P, SLOTS // 16], U16, name="offs_list")
        pos_lists = [keep.tile([P, T // 16], U16, name="pos%d_list" % r) for r in range(TOP)]

        s4_bytes = E * PASSES4 * N
        late4_bytes = 2 * N * (2 * E - AHEAD)
        first_bf = [tile([P, P, 4], BF16, "first_bf%d" % c) for c in range(2)]
        first_bf.append(held.tile([P, P, 4], BF16, name="first_bf2", align_bytes=64, offset=s4_bytes - 512))
        raw = {a: tile([P, 4, T], F32, "raw%d" % a) for a in ORDER[:-1]}
        raw[4] = spread.tile([P, 4, T], F32, name="raw4", align_bytes=64, offset=0)
        gate_rows = tile([P, T], F32, "gate_rows")
        big = {a: tile([P, 256, 4], BF16, "big%d" % a) for a in ORDER[1:]}
        small = {a: tile([P, 128, 4], BF16, "small%d" % a) for a in ORDER[1:]}
        codes = tile([P, (PASSES - 1) * T + WIDE], U32, "codes")
        planes = tile([P, 2 * T], U8, "planes")
        packed = overlay.tile([P, WIDE], U8, name="packed", align_bytes=64, offset=late4_bytes - WIDE // 2)
        words = {3: tile([P, SLOTS], U32, "words3")}
        bytes_g = tile([P, SLOTS], U8, "bytes_g")
        moved = {a: tile([P, SLOTS], U8, "moved%d" % a) for a in MOVED}
        y = [tile([P, SLOTS], F32, "y%d" % h) for h in range(HALVES)]
        prod = [[tile([P, T], F32, "prod%d_%d" % (h, r)) for r in range(TOP)] for h in range(HALVES)]
        turned = tile([P, T], F32, "turned")
        ident = tile([P, P], F32, "ident")
        res = [tile([P, T], F32, "res%d" % h) for h in range(HALVES)]
        pair = tile([P, T], F32, "pair")
        three = tile([P, T], F32, "three")
        w = {}

        def home(a):
            return T * (PASSES - 1 - ORDER.index(a))

        def load_x(a):
            nc.sync.dma_start(raw[a][:], xT[512 * a : 512 * (a + 1), :].rearrange("(p j) w -> p j w", j=4))

        def load_w4(dst, a, lo, hi):
            src = w4_words[lo:hi, a - PASSES8].rearrange("e p b -> p e b")
            nc.sync.dma_start(dst.bitcast(I32), src.bitcast(I32))

        def load_w8(dst, a, lo, hi, n0=0, n1=N):
            src = w8_words[lo:hi, a, :, n0:n1, :].rearrange("e p n r -> p e (n r)")
            nc.sync.dma_start(dst[:, :, 4 * n0 : 4 * n1].bitcast(I32), src.bitcast(I32))

        def turn(dst, src, on_vector=False):
            src = src.rearrange("p j (c i) -> p c j i", i=4)
            dst = dst[:].rearrange("p (c i) j -> p c j i", i=4)
            if on_vector:
                nc.vector.tensor_copy(out=dst, in_=src)
            else:
                nc.scalar.activation(dst, src, COPY)

        def quantise_part(a, src, lo, hi):
            at = T if a == ORDER[0] else 0
            nc.vector.quantize_mx(
                out=codes[:, home(a) + lo : home(a) + hi].bitcast(FP8X4),
                scales=planes[ROW[a] : P, at + lo : at + hi],
                in_=src[:].rearrange("p w j -> p (w j)"),
            )

        def quantise(a):
            quantise_part(a, big[a], 0, 256)
            quantise_part(a, small[a], 256, T)

        def gather_words(a, lo, hi):
            count = hi - lo
            width = 512 if count <= 384 else 1024 if count <= 768 else WIDE
            window = codes[:, home(a) : home(a) + width]
            nc.vector.tensor_copy(out=words[a][:, lo:hi], in_=window.indirect(offs_list[:, lo // 16 : hi // 16]))

        load_x(ORDER[0])
        nc.sync.dma_start(offs_list[:], offs)
        load_x(ORDER[1])
        for r, pos in enumerate((pos1, pos2, pos3, pos4)):
            nc.sync.dma_start(pos_lists[r][:], pos)
        for a in ORDER[2:]:
            load_x(a)
        nc.vector.memset(gate_rows[:], 0.0)
        nc.sync.dma_start(gate_rows[0:TOP, :], gate[:, 0, :])
        make_identity(nc, ident[:])
        nc.vector.memset(planes[:].bitcast(I32), 0)
        nc.vector.memset(packed[:].bitcast(I32), 0)
        nc.vector.memset(codes[:, PASSES * T :].bitcast(I32), 0)

        by_token = bank(2, [P, BLOCKS, P], "by_token")
        for b in range(BLOCKS):
            nc.tensor.transpose(by_token[:, b, :], gate_rows[:, P * b : P * (b + 1)], ident[:])

        for c in range(3):
            turn(first_bf[c], raw[3][:, :, P * c : P * (c + 1)], on_vector=c < 2)
        for c in range(3):
            quantise_part(3, first_bf[c], P * c, P * (c + 1))
        s8 = tile([P, PASSES8, E, N], U8, "s8", tag="raw3")
        for a in range(PASSES8):
            for r in range(4):
                src = w8_scales[:, a].rearrange("e (q r) n -> r q e n", r=4)[r]
                nc.gpsimd.dma_start(s8[ROW[a] + r : P : 32, a, :, :].bitcast(I32), src.bitcast(I32))
        for r in range(4):
            nc.sync.dma_start(packed[TOP_ROWS + r : P : 4, 0:T].bitcast(I32), planes[r:P:32, T : 2 * T].bitcast(I32))
        w[2] = held.tile([P, E, 2 * N], U8, name="w2", align_bytes=64, offset=s4_bytes)
        load_w4(w[2][:], 2, 0, E)
        s4 = held.tile([P, E * PASSES4, N], U8, name="s4", align_bytes=64, offset=0)
        for r in range(4):
            src = w4_scales.rearrange("e a (q r) n -> r q (e a) n", r=4)[r]
            nc.sync.dma_start(s4[r:P:32, :, :].bitcast(I32), src.bitcast(I32))
        for a in ORDER[1:]:
            turn(big[a], raw[a][:, :, 0:256])
            turn(small[a], raw[a][:, :, 256:T])

        gate_cols = spread.tile([P, BLOCKS, TOP], F32, name="gate_cols", align_bytes=64, offset=0)
        nc.scalar.activation(gate_cols[:], by_token[:, :, 0:TOP], COPY)
        gates = []
        for r in range(TOP - 1):
            wide = bank((7, 0, 1)[r], [P, T], "wide%d" % r)
            for b in range(BLOCKS):
                column = gate_cols[:, b, r : r + 1].to_broadcast([P, P])
                nc.tensor.transpose(wide[:, P * b : P * (b + 1)], column, ident[:])
            g = spread.tile([P, T], F32, name="gate%d" % r, align_bytes=64, offset=64 + 4 * T * r)
            nc.scalar.activation(g[:], wide[:], COPY)
            gates.append(g)

        w0_parts = [tile([P, E // 2, 4 * N], U8, "w0_%d" % i, tag="raw%d" % a) for i, a in enumerate((2, 0))]
        for i, part in enumerate(w0_parts):
            load_w8(part[:], 0, E // 2 * i, E // 2 * (i + 1))
        ahead = tile([P, AHEAD, 2 * N], U8, "ahead", tag="raw1")
        load_w4(ahead[:], 3, 0, AHEAD)

        gather_words(3, 0, SLOTS)
        words[2] = tile([P, SLOTS], U32, "words2", tag="big0")
        quantise(2)
        quantise(0)
        gather_words(2, 0, SLOTS)
        quantise(1)
        quantise(4)
        nc.vector.tensor_copy(out=packed[0:TOP_ROWS, 0:T].bitcast(I32), in_=planes[0:TOP_ROWS, 0:T].bitcast(I32))
        for lo in range(0, SLOTS, SLOTS // 2):
            hi = lo + SLOTS // 2
            nc.vector.tensor_copy(out=bytes_g[:, lo:hi], in_=packed[:].indirect(offs_list[:, lo // 16 : hi // 16]))
        for r in range(4):
            nc.sync.dma_start(moved[3][r:P:32, :].bitcast(I32), bytes_g[TOP_ROWS + r : P : 4, :].bitcast(I32))
        late4 = overlay.tile([P, 2 * E - AHEAD, 2 * N], U8, name="late4", align_bytes=64, offset=0)
        groups = [(a, lo) for a, first in ((3, AHEAD), (4, 0)) for lo in range(first, E, 4)]
        for i, (a, lo) in enumerate(groups):
            if i == len(groups) - 1:
                for r in range(4):
                    nc.sync.dma_start(moved[4][r:P:32, :].bitcast(I32), bytes_g[ROW[4] + r : P : 32, :].bitcast(I32))
            at = E * (a - 3) + lo - AHEAD
            load_w4(late4[:, at : at + 4, :], a, lo, lo + 4)
        late_words = tile([P, len(LATE), SLOTS], U32, "late_words", tag="planes")
        for i, a in enumerate(LATE):
            words[a] = late_words[:, i, :]

        banks = {}
        for h, places in enumerate(((5, 6, 7, 0, 1), (2, 3, 4))):
            for b, place in enumerate(places):
                banks[h, b] = bank(place, [P, 512], "sums%d_%d" % (h, b))
        home_bank = {(h, e): b for h in range(HALVES) for b, experts in enumerate(BANKS[h]) for e in experts}

        def product(e, h, a):
            ch = slice(P * h, P * (h + 1))
            b = home_bank[h, e]
            col = e - BANKS[h][b][0]
            s = slice(C * e, C * (e + 1))
            if a < PASSES8:
                row_of_e = w[1][:, e, :] if a == 1 else w0_parts[e // (E // 2)][:, e % (E // 2), :]
                lhsT = row_of_e[:, 4 * P * h : 4 * P * (h + 1)].bitcast(FP8X4)
                lhsT_scale = s8[ROW[a] : P, a, e, ch]
            else:
                if a == 2:
                    row_of_e = w[2][:, e, :]
                elif a == 3 and e < AHEAD:
                    row_of_e = ahead[:, e, :]
                else:
                    row_of_e = late4[:, E * (a - 3) + e - AHEAD, :]
                lhsT = row_of_e[:, 2 * P * h : 2 * P * (h + 1)].bitcast(FP4X4)
                lhsT_scale = s4[:, PASSES4 * e + a - PASSES8, ch]
            nc.tensor.matmul_mx(
                out=banks[h, b][:, C * col : C * (col + 1)],
                lhsT=lhsT,
                lhsT_scale=lhsT_scale,
                rhs=words[a][:, s].bitcast(FP8X4),
                rhs_scale=moved[a][:, s] if a in MOVED else bytes_g[ROW[a] : P, s],
                start=(a == SUM_ORDER[0] and col == 0),
                stop=(a == SUM_ORDER[-1] and e == BANKS[h][b][-1]),
            )

        def products(a):
            for lo in range(0, E, 4):
                for h in range(HALVES):
                    for e in range(lo, lo + 4):
                        product(e, h, a)

        def empty(h, b, on_vector=False):
            experts = BANKS[h][b]
            dst = y[h][:, C * experts[0] : C * (experts[-1] + 1)]
            src = banks[h, b][:, 0 : C * len(experts)]
            if on_vector:
                nc.vector.tensor_copy(out=dst, in_=src)
            else:
                nc.scalar.activation(dst, src, COPY)

        for lo in range(0, E, E // 2):
            for h in range(HALVES):
                for e in range(lo, lo + E // 2):
                    product(e, h, 2)
        w[1] = overlay.tile([P, E, 4 * N], U8, name="w1", align_bytes=64, offset=late4_bytes)
        load_w8(w[1][:, 0:WHOLE, :], 1, 0, WHOLE)
        for h, cuts in enumerate(((WHOLE, 8, 10, E), (WHOLE, 8, E))):
            for lo, hi in zip(cuts, cuts[1:]):
                load_w8(w[1][:, lo:hi, :], 1, lo, hi, P * h, P * (h + 1))
        for a in (0, 3, 4):
            if a in LATE:
                gather_words(a, 0, EARLY)
                gather_words(a, EARLY, SLOTS)
            products(a)
        last = len(BANKS[0]) - 1
        for b, experts in enumerate(BANKS[0]):
            gather_words(1, C * experts[0], C * (experts[-1] + 1))
            for e in experts:
                product(e, 0, 1)
            empty(0, b, on_vector=b == last)
            if b == 0:
                for e in experts:
                    product(e, 1, 1)
                empty(1, 0)

        def fetch_plain(h):
            nc.scalar.activation(prod[h][TOP - 1][:], y[h][:].indirect(pos_lists[TOP - 1][:]), COPY)

        def fetch(h, r, lo=0, hi=T):
            window = y[h][:].indirect(pos_lists[r][:, lo // 16 : hi // 16])
            nc.vector.tensor_tensor(prod[h][r][:, lo:hi], window, gates[r][:, lo:hi], MULT)

        blocks = [slice(P * b, P * (b + 1)) for b in range(BLOCKS)]

        def add_turned(dst, src, start, stop):
            nc.tensor.matmul(dst, src, ident[:], start=start, stop=stop, is_transpose=True)

        def gate_turned(h, place):
            plain = bank(place, [P, BLOCKS, P], "plain%d" % h)
            for b, cols in enumerate(blocks):
                nc.tensor.transpose(plain[:, b, :], prod[h][TOP - 1][:, cols], ident[:])
            for b in range(BLOCKS):
                nc.scalar.activation(gated[h][:, b, :], plain[:, b, :], COPY, scale=gate_cols[:, b, TOP - 1 : TOP])

        gated = [
            overlay.tile([P, BLOCKS, P], F32, name="gated0", align_bytes=64, offset=late4_bytes),
            tile([P, BLOCKS, P], F32, "gated1"),
        ]
        fetch_plain(0)
        for b, experts in list(enumerate(BANKS[1]))[1:]:
            for e in experts:
                product(e, 1, 1)
            empty(1, b)
        fetch_plain(1)
        gate_turned(0, 5)
        there = bank(3, [P, T], "there")
        for r in range(TOP - 1):
            fetch(0, r)
            for b, cols in enumerate(blocks):
                add_turned(there[:, cols], prod[0][r][:, cols], r == 0 and b == 0, r == TOP - 2 and b == BLOCKS - 1)
        nc.scalar.activation(turned[:], there[:], COPY)
        gate_turned(1, 6)
        back = [bank(0, [P, T], "back0"), bank(7, [P, T], "back1")]
        for b, cols in enumerate(blocks):
            add_turned(back[0][:, cols], gated[0][:, b, :], b == 0, False)
        for b, cols in enumerate(blocks):
            add_turned(back[0][:, cols], turned[:, cols], False, b == BLOCKS - 1)
        for b, cols in enumerate(blocks):
            nc.tensor.transpose(back[1][:, cols], gated[1][:, b, :], ident[:])
        nc.scalar.activation(res[0][:], back[0][:], COPY)
        nc.scalar.dma_start(out[0:P, :], res[0][:])

        pieces = ((0, 256), (256, T))
        fetch(1, 0)
        fetch(1, 1)
        fetch(1, 2, *pieces[0])
        nc.vector.tensor_tensor(pair[:], prod[1][0][:], prod[1][1][:], ADD)
        fetch(1, 2, *pieces[1])
        for lo, hi in pieces:
            nc.vector.tensor_tensor(three[:, lo:hi], pair[:, lo:hi], prod[1][2][:, lo:hi], ADD)
        for lo, hi in pieces:
            nc.vector.tensor_tensor(res[1][:, lo:hi], back[1][:, lo:hi], three[:, lo:hi], ADD)
            nc.sync.dma_start(out[P : 2 * P, lo:hi], res[1][:, lo:hi])
